import numpy as np
import ml_dtypes


def mxq(x, axis, fmt="e4m3"):
    dtype, down = {"e4m3": (ml_dtypes.float8_e4m3fn, 7), "e5m2": (ml_dtypes.float8_e5m2, 14)}[fmt]
    v = np.moveaxis(np.asarray(x, np.float32).astype(ml_dtypes.bfloat16).astype(np.float64), axis, -1)
    blocks = v.reshape(v.shape[:-1] + (-1, 32))
    amax = np.abs(blocks).max(-1, keepdims=True)
    byte = np.maximum(np.where(amax > 0, np.frexp(amax)[1] - 1 + 127, 0) - down, 1)
    scale = np.exp2(byte - 127.0)
    codes = (blocks / scale).astype(np.float32).astype(dtype).astype(np.float64)
    return np.moveaxis((codes * scale).reshape(v.shape), -1, axis)


WIDE = False


def mx_kscale(k):
    if not WIDE:
        return np.ones(k)
    levels = np.array([10, -10, 5, -5, 0])
    if k % 512:
        return np.exp2(np.random.permutation(np.resize(levels, k // 32))).repeat(32)
    a = np.empty((k // 512, 16))
    for p in range(k // 512):
        a[p, :8] = np.random.permutation(np.resize(levels, 8))
        for g in range(8):
            far = levels[np.abs(levels - a[p, g]) >= 10]
            a[p, g + 8] = far[np.random.randint(len(far))]
    return np.exp2(a.ravel()).repeat(32)


def f64(x):
    return np.asarray(x).astype(np.float64)


def striped(idx):
    return np.tile(idx.reshape(-1, 16).T, (8, 1)).astype(np.uint16)


def unstriped(offs):
    return offs[:16].T.reshape(-1).astype(np.int64)


E2M1 = np.array([0.0, 0.5, 1.0, 1.5, 2.0, 3.0, 4.0, 6.0, -0.0, -0.5, -1.0, -1.5, -2.0, -3.0, -4.0, -6.0])


def pack_weight(w, fmt):
    k, n = w.shape
    w = f64(np.asarray(w, np.float32).astype(ml_dtypes.bfloat16)).reshape(k // 32, 32, n)
    amax = np.abs(w).max(1)
    if fmt == "e4m3":
        byte = np.frexp(amax)[1] - 1 + 127 - 7
    else:
        mant, ex = np.frexp(amax / 6.0)
        byte = np.where(mant > 0.5, ex, ex - 1) + 127
    byte = np.clip(np.where(amax > 0, byte, 1), 1, 254)
    scaled = (w * np.exp2(127.0 - byte)[:, None, :]).reshape(k, n).astype(np.float32)
    by_word = np.ascontiguousarray(scaled.reshape(k // 512, 128, 4, n).transpose(0, 1, 3, 2))
    if fmt == "e4m3":
        words = by_word.astype(ml_dtypes.float8_e4m3fn).view(np.uint8)
    else:
        c = by_word.astype(ml_dtypes.float4_e2m1fn).view(np.uint8) & 0xF
        words = (c[..., 0::2] | (c[..., 1::2] << 4)).reshape(k // 512, 128, 2 * n)
    return np.ascontiguousarray(words), np.ascontiguousarray(byte.astype(np.uint8).reshape(k // 512, 16, n))


def unpack_weight(words, scales, fmt):
    g, _, n = scales.shape
    words = np.ascontiguousarray(words).reshape(g, 128, n, -1)
    if fmt == "e4m3":
        vals = words.view(ml_dtypes.float8_e4m3fn).astype(np.float64)
    else:
        nib = np.empty((g, 128, n, 4), np.uint8)
        nib[..., 0::2] = words & 0xF
        nib[..., 1::2] = words >> 4
        vals = E2M1[nib]
    vals = vals * np.repeat(np.exp2(scales.astype(np.float64) - 127.0), 8, axis=1)[..., None]
    return vals.transpose(0, 1, 3, 2).reshape(g * 512, n)


def gelu(v):
    return 0.5 * v * (1.0 + np.tanh(np.sqrt(2.0 / np.pi) * (v + 0.044715 * v**3)))


K, R, H, K2, N, T, S, TB, P = 1024, 512, 1536, 512, 512, 4096, 1024, 2048, 512

def setup_inputs():
    n = np.random.standard_normal
    s = mx_kscale(K)[:, None]
    s2 = mx_kscale(K2)[:, None]
    u = mx_kscale(H)[:, None]
    tab_words, tab_scales = pack_weight(n((K, T)) * s, "e4m3")
    tab2_words, tab2_scales = pack_weight(n((K2, TB)) * s2, "e4m3")
    w4_words, w4_scales = pack_weight(n((H, N)) / np.sqrt(H) / u, "e2m1")
    w5_words, w5_scales = pack_weight(1.5 * n((K2, N)) / np.sqrt(K2) / s2, "e4m3")
    level = np.repeat(np.array([2.5, 1.0, 0.6]), R) * np.random.uniform(0.6, 1.4, H)
    return {
        "tab_words": tab_words, "tab_scales": tab_scales,
        "offs": striped(np.random.permutation(T)[:S]),
        "tab2_words": tab2_words, "tab2_scales": tab2_scales,
        "offs2": striped(np.random.permutation(TB)[:P]),
        "pos1": striped(np.random.permutation(S)[:P]),
        "w1": (0.54 * n((K, R)) / np.sqrt(K) / s).astype(np.float32),
        "w2": (1.5 * n((K, R)) / np.sqrt(K) / s).astype(np.float32),
        "w3": (0.6 * n((K, R)) / np.sqrt(K) / s).astype(np.float32),
        "gain": (level * u[:, 0]).astype(np.float32),
        "w4_words": w4_words, "w4_scales": w4_scales,
        "w5_words": w5_words, "w5_scales": w5_scales,
        "ga": np.random.uniform(0.5, 1.5, N).astype(np.float32),
        "gb": np.random.uniform(0.5, 1.5, N).astype(np.float32),
    }

def reference(tab_words, tab_scales, offs, tab2_words, tab2_scales, offs2, pos1, w1, w2, w3, gain, w4_words, w4_scales, w5_words, w5_scales, ga, gb):
    v = unpack_weight(tab_words, tab_scales, "e4m3")[:, unstriped(offs)]
    v2 = unpack_weight(tab2_words, tab2_scales, "e4m3")[:, unstriped(offs2)]
    w4 = unpack_weight(w4_words, w4_scales, "e2m1")
    w5 = unpack_weight(w5_words, w5_scales, "e4m3")
    h1 = np.sin(mxq(f64(w1), 0, "e4m3").T @ v)
    h2 = np.tanh(mxq(f64(w2), 0, "e4m3").T @ v)
    h3 = np.exp(mxq(f64(w3), 0, "e4m3").T @ v)
    h = f64(gain)[:, None] * np.concatenate([h1, h2, h3], axis=0)
    y = w4.T @ mxq(h, 0, "e4m3")
    b = w5.T @ v2
    return np.maximum(f64(ga)[:, None] * y[:, unstriped(pos1)], f64(gb)[:, None] * b)

@@ -1,0 +1,269 @@
+import math
+from contextlib import ExitStack
+
+import concourse.mybir as mybir
+
+K, R, H, K2, N, T, S, TB, P2 = 1024, 512, 1536, 512, 512, 4096, 1024, 2048, 512
+FLOPS = 2 * (K * H * S + H * N * S + K2 * N * P2)
+
+F32 = mybir.dt.float32
+BF16 = mybir.dt.bfloat16
+I32 = mybir.dt.int32
+U32 = mybir.dt.uint32
+U16 = mybir.dt.uint16
+U8 = mybir.dt.uint8
+FP8X4 = mybir.dt.float8_e4m3fn_x4
+FP4X4 = mybir.dt.float4_e2m1fn_x4
+ACT = mybir.ActivationFunctionType
+ALU = mybir.AluOpType
+
+P = 128
+UNIT = 128
+CHUNK = 256
+HALF = 512
+TWO_PI = 2.0 * math.pi
+
+
+def tile_list_nerve_loss_warning_kernel(
+    tc, tab_words, tab_scales, offs, tab2_words, tab2_scales, offs2, pos1,
+    w1, w2, w3, gain, w4_words, w4_scales, w5_words, w5_scales, ga, gb, out,
+):
+    nc = tc.nc
+    with ExitStack() as ctx:
+        keep = ctx.enter_context(tc.tile_pool(name="keep", bufs=1))
+        planes = ctx.enter_context(tc.tile_pool(name="planes", bufs=1))
+        ring = ctx.enter_context(tc.tile_pool(name="ring", bufs=3))
+        zpool = ctx.enter_context(tc.psum_pool(name="zpool", bufs=4))
+        ypool = ctx.enter_context(tc.psum_pool(name="ypool", bufs=1))
+
+        idx = keep.tile([P, S // 16], U16, name="idx")
+        idx2 = keep.tile([P, P2 // 16], U16, name="idx2")
+        p1 = keep.tile([P, P2 // 16], U16, name="p1")
+        tw = [keep.tile([P, T], I32, name="tw%d" % a) for a in range(2)]
+        ts = planes.tile([P, T], U8, name="ts", offset=0, align_bytes=64)
+        t2s = keep.tile([P, TB], U8, name="t2s")
+        wraw = [[ring.tile([P, 4, R], F32, name="wraw%d%d" % (f, a), tag="stream", bufs=2, align_bytes=64) for a in range(2)] for f in range(3)]
+        t2w = ring.tile([P, TB], I32, name="t2w", tag="stream", bufs=2, align_bytes=64)
+        w4w = ring.tile([P, 3, 2 * N], U8, name="w4w", tag="stream", bufs=2, align_bytes=64)
+        w4s = planes.tile([P, 3, N], U8, name="w4s", offset=0, align_bytes=64)
+        w5w = ring.tile([P, N], I32, name="w5w", tag="stream", bufs=2, align_bytes=64)
+        w5s = planes.tile([P, N], U8, name="w5s", offset=3 * N, align_bytes=64)
+        gain_sb = keep.tile([P, 3, 4], F32, name="gain_sb")
+        ga_sb = planes.tile([P, 4], F32, name="ga_sb", offset=4 * N, align_bytes=64)
+        gb_sb = planes.tile([P, 4], F32, name="gb_sb", offset=4 * N + 64, align_bytes=64)
+
+        nc.sync.dma_start(idx[:], offs)
+        nc.sync.dma_start(ts[0:32, :].bitcast(I32), tab_scales.rearrange("a q t -> (a q) t").bitcast(I32))
+        nc.sync.dma_start(idx2[:], offs2)
+        nc.sync.dma_start(p1[:], pos1)
+        for a in range(2):
+            nc.sync.dma_start(tw[a][:], tab_words[a].rearrange("p t i -> p (t i)").bitcast(I32))
+        for f, w in enumerate((w1, w2, w3)):
+            for a in range(2):
+                nc.sync.dma_start(wraw[f][a][:], w[512 * a : 512 * (a + 1), :].rearrange("(p j) c -> p j c", j=4))
+        nc.sync.dma_start(t2w[:], tab2_words[0].rearrange("p t i -> p (t i)").bitcast(I32))
+        nc.sync.dma_start(w4w[:].bitcast(I32), w4_words.rearrange("a p n -> p a n").bitcast(I32))
+        nc.sync.dma_start(w5w[:], w5_words[0].rearrange("p t i -> p (t i)").bitcast(I32))
+
+        gs_rows = keep.tile([P, S], U8, name="gs_rows")
+        gs = keep.tile([P, S], U8, name="gs", align_bytes=64)
+        nc.vector.memset(t2s[:].bitcast(I32), 0)
+        nc.vector.memset(ts[32:64, :].bitcast(I32), 0)
+        nc.vector.memset(ts[64:128, :].bitcast(I32), 0)
+        nc.vector.memset(gs[:].bitcast(I32), 0)
+        nc.vector.tensor_copy(gs_rows[:], ts[:].indirect(idx[:]))
+        for a, queue in enumerate((nc.scalar, nc.gpsimd)):
+            for q in range(4):
+                queue.dma_start(
+                    gs[32 * q + 4 * a : 32 * q + 4 * a + 4, :].bitcast(I32),
+                    gs_rows[16 * a + 4 * q : 16 * a + 4 * q + 4, :].bitcast(I32),
+                )
+        nc.vector.memset(w4s[:].bitcast(I32), 0)
+        nc.vector.memset(w5s[:].bitcast(I32), 0)
+        nc.gpsimd.dma_start(gain_sb[:], gain.rearrange("(a p t) -> p a t", a=3, t=4))
+        for q in range(4):
+            nc.gpsimd.dma_start(t2s[32 * q : 32 * q + 4, :].bitcast(I32), tab2_scales[0, 4 * q : 4 * q + 4, :].bitcast(I32))
+        for q in range(4):
+            nc.gpsimd.dma_start(
+                w4s[32 * q : 32 * q + 4, :, :].bitcast(I32),
+                w4_scales[:, 4 * q : 4 * q + 4, :].rearrange("a r n -> r a n").bitcast(I32),
+            )
+        for q in range(4):
+            nc.gpsimd.dma_start(w5s[32 * q : 32 * q + 4, :].bitcast(I32), w5_scales[0, 4 * q : 4 * q + 4, :].bitcast(I32))
+        with nc.allow_non_contiguous_dma(reason="one factor to a partition"):
+            nc.gpsimd.dma_start(ga_sb[:], ga.rearrange("(c p) -> p c", p=P))
+            nc.gpsimd.dma_start(gb_sb[:], gb.rearrange("(c p) -> p c", p=P))
+
+        gw = [[keep.tile([P, HALF], U32, name="gw%d%d" % (a, h), align_bytes=64) for h in range(2)] for a in range(2)]
+        for a in range(2):
+            for h in range(2):
+                nc.vector.tensor_copy(gw[a][h][:], tw[a][:].bitcast(U32).indirect(idx[:, 32 * h : 32 * (h + 1)]))
+
+        wq = [[keep.tile([P, R], U32, name="wq%d%d" % (f, a), align_bytes=64) for a in range(2)] for f in range(3)]
+        wsc = [[keep.tile([P, R], U8, name="wsc%d%d" % (f, a), align_bytes=64) for a in range(2)] for f in range(3)]
+        wb = {}
+
+        def cast_weight(f, a, u, copy):
+            wb[f, a, u] = ring.tile([P, 2, 128, 4], BF16, name="wb", align_bytes=64, bufs=4)
+            copy(
+                wb[f, a, u][:].rearrange("p t m j -> p m j t"),
+                wraw[f][a][:].rearrange("p j (m t) -> p m j t", t=4)[:, :, :, 2 * u : 2 * u + 2],
+            )
+
+        def quantize_weight(f, a, u):
+            cols = slice(256 * u, 256 * (u + 1))
+            nc.vector.quantize_mx(
+                wq[f][a][:, cols].bitcast(FP8X4), wsc[f][a][:, cols], wb[f, a, u][:].rearrange("p t m j -> p (t m j)")
+            )
+
+        hq = [[keep.tile([P, HALF], U32, name="hq%d%d" % (f, h), align_bytes=64) for h in range(2)] for f in range(3)]
+        hs = [[keep.tile([P, HALF], U8, name="hs%d%d" % (f, h), align_bytes=64) for h in range(2)] for f in range(3)]
+        hf = {}
+        hb = {}
+
+        def first_product(f, unit):
+            z = zpool.tile([P, 4, UNIT], F32, name="z")
+            h, c0 = divmod(unit * UNIT, HALF)
+            for t in range(4):
+                for a in range(2):
+                    nc.tensor.matmul_mx(
+                        z[:, t, :],
+                        lhsT=wq[f][a][:, 128 * t : 128 * (t + 1)].bitcast(FP8X4),
+                        lhsT_scale=wsc[f][a][:, 128 * t : 128 * (t + 1)],
+                        rhs=gw[a][h][:, c0 : c0 + UNIT].bitcast(FP8X4),
+                        rhs_scale=gs[4 * a : P, unit * UNIT : (unit + 1) * UNIT],
+                        start=(a == 0),
+                        stop=(a == 1),
+                    )
+            return z[:].rearrange("p t n -> p n t")
+
+        def features(f, c):
+            zs = [first_product(f, 2 * c + e) for e in range(2)]
+            if f == 0:
+                turns = [ring.tile([P, UNIT, 4], I32, name="turns", bufs=2) for e in range(2)]
+                if c == 3:
+                    frac = keep.tile([P, CHUNK, 4], F32, name="frac_last", tag="hold")
+                else:
+                    frac = ring.tile([P, CHUNK, 4], F32, name="frac", bufs=2)
+                for e in range(2):
+                    nc.vector.tensor_scalar(turns[e][:], zs[e], 1.0 / TWO_PI, 1.0, ALU.mult, ALU.add)
+                for e in range(2):
+                    nc.vector.scalar_tensor_tensor(
+                        frac[:, UNIT * e : UNIT * (e + 1), :], zs[e], 1.0 / TWO_PI, turns[e][:], ALU.mult, ALU.subtract
+                    )
+                hf[f, c] = ring.tile([P, CHUNK, 4], F32, name="hf")
+                nc.scalar.activation(hf[f, c][:], frac[:], ACT.Sin, bias=TWO_PI, scale=TWO_PI)
+            else:
+                if (f, c) == (1, 0):
+                    hf[f, c] = keep.tile([P, CHUNK, 4], F32, name="hf_first", tag="hold")
+                else:
+                    hf[f, c] = ring.tile([P, CHUNK, 4], F32, name="hf")
+                for e in range(2):
+                    nc.scalar.activation(
+                        hf[f, c][:, UNIT * e : UNIT * (e + 1), :], zs[e], ACT.Tanh if f == 1 else ACT.Exp
+                    )
+
+        def apply_gain(f, c):
+            hb[f, c] = ring.tile([P, CHUNK, 4], BF16, name="hb", align_bytes=64)
+            nc.vector.tensor_tensor(
+                hb[f, c][:], hf[f, c][:], gain_sb[:, f : f + 1, :].to_broadcast([P, CHUNK, 4]), ALU.mult
+            )
+
+        def quantize_h(f, c):
+            h, c0 = divmod(c * CHUNK, HALF)
+            cols = slice(c0, c0 + CHUNK)
+            nc.vector.quantize_mx(
+                hq[f][h][:, cols].bitcast(FP8X4), hs[f][h][:, cols], hb[f, c][:].rearrange("p n t -> p (n t)")
+            )
+
+        ysb = [keep.tile([P, S], F32, name="ysb%d" % c) for c in range(4)]
+        ybank = {}
+
+        def second_pass(h, c, f, cols, start, stop):
+            if start:
+                ybank[h, c] = ypool.tile([P, HALF], F32, name="y%d" % c)
+            nc.tensor.matmul_mx(
+                ybank[h, c][:, cols],
+                lhsT=w4w[:, f, 256 * c : 256 * (c + 1)].bitcast(FP4X4),
+                lhsT_scale=w4s[:, f, 128 * c : 128 * (c + 1)],
+                rhs=hq[f][h][:, cols].bitcast(FP8X4),
+                rhs_scale=hs[f][h][:, cols],
+                start=start,
+                stop=stop,
+            )
+
+        def copy_y(h, c):
+            nc.scalar.activation(
+                ysb[c][:, HALF * h : HALF * (h + 1)], ybank[h, c][:], ACT.Copy, scale=ga_sb[:, c : c + 1]
+            )
+
+        whole = slice(0, HALF)
+
+        cast_weight(0, 0, 0, nc.vector.tensor_copy)
+        cast_weight(0, 0, 1, nc.vector.tensor_copy)
+        quantize_weight(0, 0, 0)
+        quantize_weight(0, 0, 1)
+        cast_weight(0, 1, 0, nc.vector.tensor_copy)
+        cast_weight(0, 1, 1, nc.scalar.copy)
+        quantize_weight(0, 1, 0)
+        quantize_weight(0, 1, 1)
+
+        order = [(0, 0), (0, 1), (0, 2), (0, 3), (1, 0), (1, 1), (2, 0), (2, 1), (1, 2), (1, 3), (2, 2), (2, 3)]
+        g2w = keep.tile([P, P2], U32, name="g2w", align_bytes=64)
+        g2s = keep.tile([P, P2], U8, name="g2s", align_bytes=64)
+        for i in range(len(order) + 2):
+            if i < len(order):
+                features(*order[i])
+            if 1 <= i <= len(order):
+                apply_gain(*order[i - 1])
+            if i >= 2:
+                quantize_h(*order[i - 2])
+            if i < 4:
+                f, a = 1 + i // 2, i % 2
+                for u in range(2):
+                    cast_weight(f, a, u, nc.scalar.copy)
+                for u in range(2):
+                    quantize_weight(f, a, u)
+            if i == 9:
+                for c in range(4):
+                    for f in range(3):
+                        second_pass(0, c, f, whole, f == 0, f == 2)
+                    copy_y(0, c)
+            if i == 11:
+                for c in range(4):
+                    second_pass(1, c, 0, whole, True, False)
+                    second_pass(1, c, 1, whole, False, False)
+            if i == 12:
+                for c in range(4):
+                    second_pass(1, c, 2, slice(0, CHUNK), False, False)
+        for c in range(4):
+            second_pass(1, c, 2, slice(CHUNK, HALF), False, True)
+            copy_y(1, c)
+
+        nc.vector.tensor_copy(g2s[:], t2s[:].indirect(idx2[:]))
+        nc.vector.tensor_copy(g2w[:], t2w[:].bitcast(U32).indirect(idx2[:]))
+        picked = []
+        bbank = []
+        for c in range(4):
+            b = zpool.tile([P, P2], F32, name="z")
+            nc.tensor.matmul_mx(
+                b[:],
+                lhsT=w5w[:, 128 * c : 128 * (c + 1)].bitcast(FP8X4),
+                lhsT_scale=w5s[:, 128 * c : 128 * (c + 1)],
+                rhs=g2w[:].bitcast(FP8X4),
+                rhs_scale=g2s[:],
+                start=True,
+                stop=True,
+            )
+            bbank.append(b)
+        for c in range(5):
+            if c < 4:
+                pk = ring.tile([P, P2], F32, name="pk")
+                nc.vector.tensor_copy(pk[:], ysb[c][:].indirect(p1[:]))
+                picked.append(pk)
+            if c >= 1:
+                res = keep.tile([P, P2], F32, name="res%d" % (c - 1))
+                nc.vector.scalar_tensor_tensor(
+                    res[:], bbank[c - 1][:], gb_sb[:, c - 1 : c], picked[c - 1][:], ALU.mult, ALU.max
+                )
+                nc.sync.dma_start(out[128 * (c - 1) : 128 * c, :], res[:])

@@ -39,18 +39,20 @@ def tile_list_nerve_loss_warning_kernel(
         idx = keep.tile([P, S // 16], U16, name="idx")
         idx2 = keep.tile([P, P2 // 16], U16, name="idx2")
         p1 = keep.tile([P, P2 // 16], U16, name="p1")
-        tw = [keep.tile([P, T], I32, name="tw%d" % a) for a in range(2)]
-        ts = planes.tile([P, T], U8, name="ts", offset=0, align_bytes=64)
+        tw = [planes.tile([P, T], I32, name="tw%d" % a, offset=4 * T * a, align_bytes=64) for a in range(2)]
+        ts = keep.tile([P, T], U8, name="ts")
         t2s = keep.tile([P, TB], U8, name="t2s")
-        wraw = [[ring.tile([P, 4, R], F32, name="wraw%d%d" % (f, a), tag="stream", bufs=2, align_bytes=64) for a in range(2)] for f in range(3)]
-        t2w = ring.tile([P, TB], I32, name="t2w", tag="stream", bufs=2, align_bytes=64)
-        w4w = ring.tile([P, 3, 2 * N], U8, name="w4w", tag="stream", bufs=2, align_bytes=64)
-        w4s = planes.tile([P, 3, N], U8, name="w4s", offset=0, align_bytes=64)
-        w5w = ring.tile([P, N], I32, name="w5w", tag="stream", bufs=2, align_bytes=64)
-        w5s = planes.tile([P, N], U8, name="w5s", offset=3 * N, align_bytes=64)
         gain_sb = keep.tile([P, 3, 4], F32, name="gain_sb")
-        ga_sb = planes.tile([P, 4], F32, name="ga_sb", offset=4 * N, align_bytes=64)
-        gb_sb = planes.tile([P, 4], F32, name="gb_sb", offset=4 * N + 64, align_bytes=64)
+
+        def stream_tile(shape, dtype, name):
+            return ring.tile(shape, dtype, name=name, tag="stream", bufs=3, align_bytes=64)
+
+        wraw = {}
+
+        def load_weight(f, a):
+            w = (w1, w2, w3)[f]
+            wraw[f, a] = stream_tile([P, 4, R], F32, "wraw%d%d" % (f, a))
+            nc.sync.dma_start(wraw[f, a][:], w[512 * a : 512 * (a + 1), :].rearrange("(p j) c -> p j c", j=4))
 
         nc.sync.dma_start(idx[:], offs)
         nc.sync.dma_start(ts[0:32, :].bitcast(I32), tab_scales.rearrange("a q t -> (a q) t").bitcast(I32))
@@ -58,11 +60,16 @@ def tile_list_nerve_loss_warning_kernel(
         nc.sync.dma_start(p1[:], pos1)
         for a in range(2):
             nc.sync.dma_start(tw[a][:], tab_words[a].rearrange("p t i -> p (t i)").bitcast(I32))
-        for f, w in enumerate((w1, w2, w3)):
+        for f in range(2):
             for a in range(2):
-                nc.sync.dma_start(wraw[f][a][:], w[512 * a : 512 * (a + 1), :].rearrange("(p j) c -> p j c", j=4))
-        nc.sync.dma_start(t2w[:], tab2_words[0].rearrange("p t i -> p (t i)").bitcast(I32))
+                load_weight(f, a)
+        w4w = stream_tile([P, 3, 2 * N], U8, "w4w")
         nc.sync.dma_start(w4w[:].bitcast(I32), w4_words.rearrange("a p n -> p a n").bitcast(I32))
+        for a in range(2):
+            load_weight(2, a)
+        t2w = stream_tile([P, TB], I32, "t2w")
+        nc.sync.dma_start(t2w[:], tab2_words[0].rearrange("p t i -> p (t i)").bitcast(I32))
+        w5w = stream_tile([P, N], I32, "w5w")
         nc.sync.dma_start(w5w[:], w5_words[0].rearrange("p t i -> p (t i)").bitcast(I32))
 
         gs_rows = keep.tile([P, S], U8, name="gs_rows")
@@ -78,26 +85,31 @@ def tile_list_nerve_loss_warning_kernel(
                     gs[32 * q + 4 * a : 32 * q + 4 * a + 4, :].bitcast(I32),
                     gs_rows[16 * a + 4 * q : 16 * a + 4 * q + 4, :].bitcast(I32),
                 )
-        nc.vector.memset(w4s[:].bitcast(I32), 0)
-        nc.vector.memset(w5s[:].bitcast(I32), 0)
-        nc.gpsimd.dma_start(gain_sb[:], gain.rearrange("(a p t) -> p a t", a=3, t=4))
         for q in range(4):
             nc.gpsimd.dma_start(t2s[32 * q : 32 * q + 4, :].bitcast(I32), tab2_scales[0, 4 * q : 4 * q + 4, :].bitcast(I32))
-        for q in range(4):
-            nc.gpsimd.dma_start(
-                w4s[32 * q : 32 * q + 4, :, :].bitcast(I32),
-                w4_scales[:, 4 * q : 4 * q + 4, :].rearrange("a r n -> r a n").bitcast(I32),
-            )
-        for q in range(4):
-            nc.gpsimd.dma_start(w5s[32 * q : 32 * q + 4, :].bitcast(I32), w5_scales[0, 4 * q : 4 * q + 4, :].bitcast(I32))
-        with nc.allow_non_contiguous_dma(reason="one factor to a partition"):
-            nc.gpsimd.dma_start(ga_sb[:], ga.rearrange("(c p) -> p c", p=P))
-            nc.gpsimd.dma_start(gb_sb[:], gb.rearrange("(c p) -> p c", p=P))
+        nc.gpsimd.dma_start(gain_sb[:], gain.rearrange("(a p t) -> p a t", a=3, t=4))
 
         gw = [[keep.tile([P, HALF], U32, name="gw%d%d" % (a, h), align_bytes=64) for h in range(2)] for a in range(2)]
         for a in range(2):
             for h in range(2):
                 nc.vector.tensor_copy(gw[a][h][:], tw[a][:].bitcast(U32).indirect(idx[:, 32 * h : 32 * (h + 1)]))
+
+        w4s = planes.tile([P, 3, N], U8, name="w4s", offset=4 * T, align_bytes=64)
+        w5s = planes.tile([P, N], U8, name="w5s", offset=4 * T + 3 * N, align_bytes=64)
+        ga_sb = planes.tile([P, 4], F32, name="ga_sb", offset=4 * T + 4 * N, align_bytes=64)
+        gb_sb = planes.tile([P, 4], F32, name="gb_sb", offset=4 * T + 4 * N + 64, align_bytes=64)
+        nc.gpsimd.memset(w4s[:].bitcast(I32), 0)
+        nc.gpsimd.memset(w5s[:].bitcast(I32), 0)
+        for q in range(4):
+            nc.sync.dma_start(
+                w4s[32 * q : 32 * q + 4, :, :].bitcast(I32),
+                w4_scales[:, 4 * q : 4 * q + 4, :].rearrange("a r n -> r a n").bitcast(I32),
+            )
+        for q in range(4):
+            nc.sync.dma_start(w5s[32 * q : 32 * q + 4, :].bitcast(I32), w5_scales[0, 4 * q : 4 * q + 4, :].bitcast(I32))
+        with nc.allow_non_contiguous_dma(reason="one factor to a partition"):
+            nc.sync.dma_start(ga_sb[:], ga.rearrange("(c p) -> p c", p=P))
+            nc.sync.dma_start(gb_sb[:], gb.rearrange("(c p) -> p c", p=P))
 
         wq = [[keep.tile([P, R], U32, name="wq%d%d" % (f, a), align_bytes=64) for a in range(2)] for f in range(3)]
         wsc = [[keep.tile([P, R], U8, name="wsc%d%d" % (f, a), align_bytes=64) for a in range(2)] for f in range(3)]
@@ -107,7 +119,7 @@ def tile_list_nerve_loss_warning_kernel(
             wb[f, a, u] = ring.tile([P, 2, 128, 4], BF16, name="wb", align_bytes=64, bufs=4)
             copy(
                 wb[f, a, u][:].rearrange("p t m j -> p m j t"),
-                wraw[f][a][:].rearrange("p j (m t) -> p m j t", t=4)[:, :, :, 2 * u : 2 * u + 2],
+                wraw[f, a][:].rearrange("p j (m t) -> p m j t", t=4)[:, :, :, 2 * u : 2 * u + 2],
             )
 
         def quantize_weight(f, a, u):
@@ -124,16 +136,16 @@ def tile_list_nerve_loss_warning_kernel(
         def first_product(f, unit):
             z = zpool.tile([P, 4, UNIT], F32, name="z")
             h, c0 = divmod(unit * UNIT, HALF)
-            for t in range(4):
-                for a in range(2):
+            for a in range(2):
+                for t in range(4):
                     nc.tensor.matmul_mx(
                         z[:, t, :],
                         lhsT=wq[f][a][:, 128 * t : 128 * (t + 1)].bitcast(FP8X4),
                         lhsT_scale=wsc[f][a][:, 128 * t : 128 * (t + 1)],
                         rhs=gw[a][h][:, c0 : c0 + UNIT].bitcast(FP8X4),
                         rhs_scale=gs[4 * a : P, unit * UNIT : (unit + 1) * UNIT],
-                        start=(a == 0),
-                        stop=(a == 1),
+                        start=(a == 0 and t == 0),
+                        stop=(a == 1 and t == 3),
                     )
             return z[:].rearrange("p t n -> p n t")
 
@@ -146,18 +158,18 @@ def tile_list_nerve_loss_warning_kernel(
                 else:
                     frac = ring.tile([P, CHUNK, 4], F32, name="frac", bufs=2)
                 for e in range(2):
-                    nc.vector.tensor_scalar(turns[e][:], zs[e], 1.0 / TWO_PI, 1.0, ALU.mult, ALU.add)
+                    nc.vector.tensor_scalar(turns[e][:], zs[e], 1.0 / TWO_PI, None, ALU.mult)
                 for e in range(2):
                     nc.vector.scalar_tensor_tensor(
                         frac[:, UNIT * e : UNIT * (e + 1), :], zs[e], 1.0 / TWO_PI, turns[e][:], ALU.mult, ALU.subtract
                     )
-                hf[f, c] = ring.tile([P, CHUNK, 4], F32, name="hf")
-                nc.scalar.activation(hf[f, c][:], frac[:], ACT.Sin, bias=TWO_PI, scale=TWO_PI)
+                hf[f, c] = ring.tile([P, CHUNK, 4], F32, name="hf", bufs=4)
+                nc.scalar.activation(hf[f, c][:], frac[:], ACT.Sin, scale=TWO_PI)
             else:
                 if (f, c) == (1, 0):
                     hf[f, c] = keep.tile([P, CHUNK, 4], F32, name="hf_first", tag="hold")
                 else:
-                    hf[f, c] = ring.tile([P, CHUNK, 4], F32, name="hf")
+                    hf[f, c] = ring.tile([P, CHUNK, 4], F32, name="hf", bufs=4)
                 for e in range(2):
                     nc.scalar.activation(
                         hf[f, c][:, UNIT * e : UNIT * (e + 1), :], zs[e], ACT.Tanh if f == 1 else ACT.Exp
@@ -165,7 +177,8 @@ def tile_list_nerve_loss_warning_kernel(
 
         def apply_gain(f, c):
             hb[f, c] = ring.tile([P, CHUNK, 4], BF16, name="hb", align_bytes=64)
-            nc.vector.tensor_tensor(
+            engine = nc.gpsimd if f == 0 else nc.vector
+            engine.tensor_tensor(
                 hb[f, c][:], hf[f, c][:], gain_sb[:, f : f + 1, :].to_broadcast([P, CHUNK, 4]), ALU.mult
             )
 
@@ -181,7 +194,10 @@ def tile_list_nerve_loss_warning_kernel(
 
         def second_pass(h, c, f, cols, start, stop):
             if start:
-                ybank[h, c] = ypool.tile([P, HALF], F32, name="y%d" % c)
+                if h == 0:
+                    ybank[h, c] = ypool.tile([P, HALF], F32, name="y%d" % c)
+                else:
+                    ybank[h, c] = zpool.tile([P, HALF], F32, name="z")
             nc.tensor.matmul_mx(
                 ybank[h, c][:, cols],
                 lhsT=w4w[:, f, 256 * c : 256 * (c + 1)].bitcast(FP4X4),
@@ -208,7 +224,7 @@ def tile_list_nerve_loss_warning_kernel(
         quantize_weight(0, 1, 0)
         quantize_weight(0, 1, 1)
 
-        order = [(0, 0), (0, 1), (0, 2), (0, 3), (1, 0), (1, 1), (2, 0), (2, 1), (1, 2), (1, 3), (2, 2), (2, 3)]
+        order = [(f, c) for f in range(3) for c in range(4)]
         g2w = keep.tile([P, P2], U32, name="g2w", align_bytes=64)
         g2s = keep.tile([P, P2], U8, name="g2s", align_bytes=64)
         for i in range(len(order) + 2):
@@ -224,20 +240,21 @@ def tile_list_nerve_loss_warning_kernel(
                     cast_weight(f, a, u, nc.scalar.copy)
                 for u in range(2):
                     quantize_weight(f, a, u)
-            if i == 9:
+            if i >= 2 and order[i - 2][1] == 1:
+                f = order[i - 2][0]
                 for c in range(4):
-                    for f in range(3):
-                        second_pass(0, c, f, whole, f == 0, f == 2)
-                    copy_y(0, c)
+                    second_pass(0, c, f, whole, f == 0, f == 2)
             if i == 11:
+                copy_y(0, 0)
+            if i == 12:
                 for c in range(4):
                     second_pass(1, c, 0, whole, True, False)
                     second_pass(1, c, 1, whole, False, False)
-            if i == 12:
-                for c in range(4):
                     second_pass(1, c, 2, slice(0, CHUNK), False, False)
         for c in range(4):
             second_pass(1, c, 2, slice(CHUNK, HALF), False, True)
+            if c > 0:
+                copy_y(0, c)
             copy_y(1, c)
 
         nc.vector.tensor_copy(g2s[:], t2s[:].indirect(idx2[:]))
@@ -245,7 +262,7 @@ def tile_list_nerve_loss_warning_kernel(
         picked = []
         bbank = []
         for c in range(4):
-            b = zpool.tile([P, P2], F32, name="z")
+            b = ypool.tile([P, P2], F32, name="y%d" % c)
             nc.tensor.matmul_mx(
                 b[:],
                 lhsT=w5w[:, 128 * c : 128 * (c + 1)].bitcast(FP8X4),

@@ -21,6 +21,7 @@ P = 128
 UNIT = 128
 CHUNK = 256
 HALF = 512
+SLOT = 8192
 TWO_PI = 2.0 * math.pi
 
 
@@ -39,20 +40,15 @@ def tile_list_nerve_loss_warning_kernel(
         idx = keep.tile([P, S // 16], U16, name="idx")
         idx2 = keep.tile([P, P2 // 16], U16, name="idx2")
         p1 = keep.tile([P, P2 // 16], U16, name="p1")
-        tw = [planes.tile([P, T], I32, name="tw%d" % a, offset=4 * T * a, align_bytes=64) for a in range(2)]
-        ts = keep.tile([P, T], U8, name="ts")
-        t2s = keep.tile([P, TB], U8, name="t2s")
+        def placed(shape, dtype, name, offset):
+            return planes.tile(shape, dtype, name=name, offset=offset, align_bytes=64)
+
+        slot = [8 * T, 8 * T + SLOT, 0]
+        tw = [placed([P, T], I32, "tw%d" % a, 4 * T * a) for a in range(2)]
+        ts = placed([P, T], U8, "ts", slot[1] - T // 2)
         gain_sb = keep.tile([P, 3, 4], F32, name="gain_sb")
-
-        def stream_tile(shape, dtype, name):
-            return ring.tile(shape, dtype, name=name, tag="stream", bufs=3, align_bytes=64)
-
-        wraw = {}
-
-        def load_weight(f, a):
-            w = (w1, w2, w3)[f]
-            wraw[f, a] = stream_tile([P, 4, R], F32, "wraw%d%d" % (f, a))
-            nc.sync.dma_start(wraw[f, a][:], w[512 * a : 512 * (a + 1), :].rearrange("(p j) c -> p j c", j=4))
+        gs_rows = keep.tile([P, S], U8, name="gs_rows")
+        gs = keep.tile([P, S], U8, name="gs", align_bytes=64)
 
         nc.sync.dma_start(idx[:], offs)
         nc.sync.dma_start(ts[0:32, :].bitcast(I32), tab_scales.rearrange("a q t -> (a q) t").bitcast(I32))
@@ -60,21 +56,10 @@ def tile_list_nerve_loss_warning_kernel(
         nc.sync.dma_start(p1[:], pos1)
         for a in range(2):
             nc.sync.dma_start(tw[a][:], tab_words[a].rearrange("p t i -> p (t i)").bitcast(I32))
-        for f in range(2):
-            for a in range(2):
-                load_weight(f, a)
-        w4w = stream_tile([P, 3, 2 * N], U8, "w4w")
-        nc.sync.dma_start(w4w[:].bitcast(I32), w4_words.rearrange("a p n -> p a n").bitcast(I32))
-        for a in range(2):
-            load_weight(2, a)
-        t2w = stream_tile([P, TB], I32, "t2w")
-        nc.sync.dma_start(t2w[:], tab2_words[0].rearrange("p t i -> p (t i)").bitcast(I32))
-        w5w = stream_tile([P, N], I32, "w5w")
-        nc.sync.dma_start(w5w[:], w5_words[0].rearrange("p t i -> p (t i)").bitcast(I32))
+        nc.sync.dma_start(gain_sb[:], gain.rearrange("(a p t) -> p a t", a=3, t=4))
 
-        gs_rows = keep.tile([P, S], U8, name="gs_rows")
-        gs = keep.tile([P, S], U8, name="gs", align_bytes=64)
-        nc.vector.memset(t2s[:].bitcast(I32), 0)
+        t2s = keep.tile([P, TB], U8, name="t2s")
+        nc.gpsimd.memset(t2s[:].bitcast(I32), 0)
         nc.vector.memset(ts[32:64, :].bitcast(I32), 0)
         nc.vector.memset(ts[64:128, :].bitcast(I32), 0)
         nc.vector.memset(gs[:].bitcast(I32), 0)
@@ -85,31 +70,38 @@ def tile_list_nerve_loss_warning_kernel(
                     gs[32 * q + 4 * a : 32 * q + 4 * a + 4, :].bitcast(I32),
                     gs_rows[16 * a + 4 * q : 16 * a + 4 * q + 4, :].bitcast(I32),
                 )
+
         for q in range(4):
             nc.gpsimd.dma_start(t2s[32 * q : 32 * q + 4, :].bitcast(I32), tab2_scales[0, 4 * q : 4 * q + 4, :].bitcast(I32))
-        nc.gpsimd.dma_start(gain_sb[:], gain.rearrange("(a p t) -> p a t", a=3, t=4))
+
+        wraw = {}
+
+        def load_weight(f, a):
+            w = (w1, w2, w3)[f]
+            wraw[f, a] = placed([P, 4, R], F32, "wraw%d%d" % (f, a), slot[(2 * f + a) % 3])
+            nc.sync.dma_start(wraw[f, a][:], w[512 * a : 512 * (a + 1), :].rearrange("(p j) c -> p j c", j=4))
+
+        load_weight(0, 0)
+        load_weight(0, 1)
 
         gw = [[keep.tile([P, HALF], U32, name="gw%d%d" % (a, h), align_bytes=64) for h in range(2)] for a in range(2)]
         for a in range(2):
             for h in range(2):
                 nc.vector.tensor_copy(gw[a][h][:], tw[a][:].bitcast(U32).indirect(idx[:, 32 * h : 32 * (h + 1)]))
+            if a == 0:
+                g2s = placed([P, P2], U8, "g2s", SLOT + 8 * N)
+                nc.vector.tensor_copy(g2s[:], t2s[:].indirect(idx2[:]))
 
-        w4s = planes.tile([P, 3, N], U8, name="w4s", offset=4 * T, align_bytes=64)
-        w5s = planes.tile([P, N], U8, name="w5s", offset=4 * T + 3 * N, align_bytes=64)
-        ga_sb = planes.tile([P, 4], F32, name="ga_sb", offset=4 * T + 4 * N, align_bytes=64)
-        gb_sb = planes.tile([P, 4], F32, name="gb_sb", offset=4 * T + 4 * N + 64, align_bytes=64)
+        load_weight(1, 0)
+        w4w = placed([P, 3, 2 * N], U8, "w4w", SLOT)
+        nc.sync.dma_start(w4w[:].bitcast(I32), w4_words.rearrange("a p n -> p a n").bitcast(I32))
+        w4s = placed([P, 3, N], U8, "w4s", 4 * T)
         nc.gpsimd.memset(w4s[:].bitcast(I32), 0)
-        nc.gpsimd.memset(w5s[:].bitcast(I32), 0)
         for q in range(4):
             nc.sync.dma_start(
                 w4s[32 * q : 32 * q + 4, :, :].bitcast(I32),
                 w4_scales[:, 4 * q : 4 * q + 4, :].rearrange("a r n -> r a n").bitcast(I32),
             )
-        for q in range(4):
-            nc.sync.dma_start(w5s[32 * q : 32 * q + 4, :].bitcast(I32), w5_scales[0, 4 * q : 4 * q + 4, :].bitcast(I32))
-        with nc.allow_non_contiguous_dma(reason="one factor to a partition"):
-            nc.sync.dma_start(ga_sb[:], ga.rearrange("(c p) -> p c", p=P))
-            nc.sync.dma_start(gb_sb[:], gb.rearrange("(c p) -> p c", p=P))
 
         wq = [[keep.tile([P, R], U32, name="wq%d%d" % (f, a), align_bytes=64) for a in range(2)] for f in range(3)]
         wsc = [[keep.tile([P, R], U8, name="wsc%d%d" % (f, a), align_bytes=64) for a in range(2)] for f in range(3)]
@@ -152,11 +144,11 @@ def tile_list_nerve_loss_warning_kernel(
         def features(f, c):
             zs = [first_product(f, 2 * c + e) for e in range(2)]
             if f == 0:
-                turns = [ring.tile([P, UNIT, 4], I32, name="turns", bufs=2) for e in range(2)]
+                turns = [ring.tile([P, UNIT, 4], I32, name="turns", bufs=4) for e in range(2)]
                 if c == 3:
                     frac = keep.tile([P, CHUNK, 4], F32, name="frac_last", tag="hold")
                 else:
-                    frac = ring.tile([P, CHUNK, 4], F32, name="frac", bufs=2)
+                    frac = ring.tile([P, CHUNK, 4], F32, name="frac", bufs=3)
                 for e in range(2):
                     nc.vector.tensor_scalar(turns[e][:], zs[e], 1.0 / TWO_PI, None, ALU.mult)
                 for e in range(2):
@@ -216,17 +208,18 @@ def tile_list_nerve_loss_warning_kernel(
         whole = slice(0, HALF)
 
         cast_weight(0, 0, 0, nc.vector.tensor_copy)
-        cast_weight(0, 0, 1, nc.vector.tensor_copy)
+        cast_weight(0, 0, 1, nc.scalar.copy)
+        load_weight(1, 1)
         quantize_weight(0, 0, 0)
         quantize_weight(0, 0, 1)
         cast_weight(0, 1, 0, nc.vector.tensor_copy)
         cast_weight(0, 1, 1, nc.scalar.copy)
+        load_weight(2, 0)
         quantize_weight(0, 1, 0)
         quantize_weight(0, 1, 1)
 
         order = [(f, c) for f in range(3) for c in range(4)]
         g2w = keep.tile([P, P2], U32, name="g2w", align_bytes=64)
-        g2s = keep.tile([P, P2], U8, name="g2s", align_bytes=64)
         for i in range(len(order) + 2):
             if i < len(order):
                 features(*order[i])
@@ -238,6 +231,26 @@ def tile_list_nerve_loss_warning_kernel(
                 f, a = 1 + i // 2, i % 2
                 for u in range(2):
                     cast_weight(f, a, u, nc.scalar.copy)
+                if i == 0:
+                    load_weight(2, 1)
+                if i == 1:
+                    t2w = placed([P, TB], I32, "t2w", slot[0])
+                    nc.sync.dma_start(t2w[:], tab2_words[0].rearrange("p t i -> p (t i)").bitcast(I32))
+                if i == 2:
+                    w5w = placed([P, N], I32, "w5w", slot[1])
+                    nc.sync.dma_start(w5w[:], w5_words[0].rearrange("p t i -> p (t i)").bitcast(I32))
+                if i == 3:
+                    w5s = placed([P, N], U8, "w5s", slot[2] + TB)
+                    ga_sb = placed([P, 4], F32, "ga_sb", slot[2] + TB + N)
+                    gb_sb = placed([P, 4], F32, "gb_sb", slot[2] + TB + N + 64)
+                    nc.gpsimd.memset(w5s[:].bitcast(I32), 0)
+                    with nc.allow_non_contiguous_dma(reason="one factor to a partition"):
+                        nc.sync.dma_start(ga_sb[:], ga.rearrange("(c p) -> p c", p=P))
+                        nc.sync.dma_start(gb_sb[:], gb.rearrange("(c p) -> p c", p=P))
+                    for q in range(4):
+                        nc.sync.dma_start(
+                            w5s[32 * q : 32 * q + 4, :].bitcast(I32), w5_scales[0, 4 * q : 4 * q + 4, :].bitcast(I32)
+                        )
                 for u in range(2):
                     quantize_weight(f, a, u)
             if i >= 2 and order[i - 2][1] == 1:
@@ -257,7 +270,6 @@ def tile_list_nerve_loss_warning_kernel(
                 copy_y(0, c)
             copy_y(1, c)
 
-        nc.vector.tensor_copy(g2s[:], t2s[:].indirect(idx2[:]))
         nc.vector.tensor_copy(g2w[:], t2w[:].bitcast(U32).indirect(idx2[:]))
         picked = []
         bbank = []
@@ -273,14 +285,17 @@ def tile_list_nerve_loss_warning_kernel(
                 stop=True,
             )
             bbank.append(b)
-        for c in range(5):
-            if c < 4:
-                pk = ring.tile([P, P2], F32, name="pk")
-                nc.vector.tensor_copy(pk[:], ysb[c][:].indirect(p1[:]))
+        pieces = [(0, 0, P2), (1, 0, P2), (2, 0, P2), (3, 0, P2 // 2), (3, P2 // 2, P2)]
+        for i in range(len(pieces) + 1):
+            if i < len(pieces):
+                c, j0, j1 = pieces[i]
+                pk = ring.tile([P, j1 - j0], F32, name="pk")
+                nc.vector.tensor_copy(pk[:], ysb[c][:].indirect(p1[:, j0 // 16 : j1 // 16]))
                 picked.append(pk)
-            if c >= 1:
-                res = keep.tile([P, P2], F32, name="res%d" % (c - 1))
+            if i >= 1:
+                c, j0, j1 = pieces[i - 1]
+                res = keep.tile([P, j1 - j0], F32, name="res%d" % (i - 1))
                 nc.vector.scalar_tensor_tensor(
-                    res[:], bbank[c - 1][:], gb_sb[:, c - 1 : c], picked[c - 1][:], ALU.mult, ALU.max
+                    res[:], bbank[c][:, j0:j1], gb_sb[:, c : c + 1], picked[i - 1][:], ALU.mult, ALU.max
                 )
-                nc.sync.dma_start(out[128 * (c - 1) : 128 * c, :], res[:])
+                nc.sync.dma_start(out[128 * c : 128 * (c + 1), j0:j1], res[:])

@@ -46,7 +46,7 @@ def tile_list_nerve_loss_warning_kernel(
         slot = [8 * T, 8 * T + SLOT, 0]
         tw = [placed([P, T], I32, "tw%d" % a, 4 * T * a) for a in range(2)]
         ts = placed([P, T], U8, "ts", slot[1] - T // 2)
-        gain_sb = keep.tile([P, 3, 4], F32, name="gain_sb")
+        gain_sb = keep.tile([P, 3, 2, 2], F32, name="gain_sb")
         gs_rows = keep.tile([P, S], U8, name="gs_rows")
         gs = keep.tile([P, S], U8, name="gs", align_bytes=64)
 
@@ -56,7 +56,7 @@ def tile_list_nerve_loss_warning_kernel(
         nc.sync.dma_start(p1[:], pos1)
         for a in range(2):
             nc.sync.dma_start(tw[a][:], tab_words[a].rearrange("p t i -> p (t i)").bitcast(I32))
-        nc.sync.dma_start(gain_sb[:], gain.rearrange("(a p t) -> p a t", a=3, t=4))
+        nc.sync.dma_start(gain_sb[:], gain.rearrange("(a p u e) -> p a u e", a=3, u=2, e=2))
 
         t2s = keep.tile([P, TB], U8, name="t2s")
         nc.gpsimd.memset(t2s[:].bitcast(I32), 0)
@@ -108,16 +108,21 @@ def tile_list_nerve_loss_warning_kernel(
         wb = {}
 
         def cast_weight(f, a, u, copy):
-            wb[f, a, u] = ring.tile([P, 2, 128, 4], BF16, name="wb", align_bytes=64, bufs=4)
-            copy(
-                wb[f, a, u][:].rearrange("p t m j -> p m j t"),
-                wraw[f, a][:].rearrange("p j (m t) -> p m j t", t=4)[:, :, :, 2 * u : 2 * u + 2],
-            )
+            if u == 0:
+                wb[f, a] = ring.tile([P, 4, 128, 4], BF16, name="wb", align_bytes=64, bufs=3)
+            dst = wb[f, a][:, 2 * u : 2 * u + 2]
+            src = wraw[f, a][:].rearrange("p j (m t) -> p j m t", t=4)[:, :, :, 2 * u : 2 * u + 2]
+            if copy is None:
+                nc.gpsimd.tensor_scalar(
+                    dst.rearrange("p t m j -> p m t j"), src.rearrange("p j m t -> p m t j"), 1.0, 0.0, ALU.mult, ALU.add
+                )
+            else:
+                copy(dst.rearrange("p t m j -> p m j t"), src.rearrange("p j m t -> p m j t"))
 
-        def quantize_weight(f, a, u):
-            cols = slice(256 * u, 256 * (u + 1))
+        def quantize_weight(f, a, t0, t1):
+            cols = slice(128 * t0, 128 * t1)
             nc.vector.quantize_mx(
-                wq[f][a][:, cols].bitcast(FP8X4), wsc[f][a][:, cols], wb[f, a, u][:].rearrange("p t m j -> p (t m j)")
+                wq[f][a][:, cols].bitcast(FP8X4), wsc[f][a][:, cols], wb[f, a][:, t0:t1].rearrange("p t m j -> p (t m j)")
             )
 
         hq = [[keep.tile([P, HALF], U32, name="hq%d%d" % (f, h), align_bytes=64) for h in range(2)] for f in range(3)]
@@ -125,60 +130,65 @@ def tile_list_nerve_loss_warning_kernel(
         hf = {}
         hb = {}
 
-        def first_product(f, unit):
-            z = zpool.tile([P, 4, UNIT], F32, name="z")
-            h, c0 = divmod(unit * UNIT, HALF)
+        def first_product(f, c, u):
+            z = zpool.tile([P, 2, CHUNK], F32, name="z")
+            h, c0 = divmod(c * CHUNK, HALF)
             for a in range(2):
-                for t in range(4):
+                for e in range(2):
+                    t = 2 * u + e
                     nc.tensor.matmul_mx(
-                        z[:, t, :],
+                        z[:, e, :],
                         lhsT=wq[f][a][:, 128 * t : 128 * (t + 1)].bitcast(FP8X4),
                         lhsT_scale=wsc[f][a][:, 128 * t : 128 * (t + 1)],
-                        rhs=gw[a][h][:, c0 : c0 + UNIT].bitcast(FP8X4),
-                        rhs_scale=gs[4 * a : P, unit * UNIT : (unit + 1) * UNIT],
-                        start=(a == 0 and t == 0),
-                        stop=(a == 1 and t == 3),
+                        rhs=gw[a][h][:, c0 : c0 + CHUNK].bitcast(FP8X4),
+                        rhs_scale=gs[4 * a : P, c * CHUNK : (c + 1) * CHUNK],
+                        start=(a == 0 and e == 0),
+                        stop=(a == 1 and e == 1),
                     )
-            return z[:].rearrange("p t n -> p n t")
+            return z[:].rearrange("p e n -> p n e")
 
         def features(f, c):
-            zs = [first_product(f, 2 * c + e) for e in range(2)]
+            zs = [first_product(f, c, u) for u in range(2)]
             if f == 0:
-                turns = [ring.tile([P, UNIT, 4], I32, name="turns", bufs=4) for e in range(2)]
+                turns = [ring.tile([P, CHUNK, 2], I32, name="turns", bufs=4) for u in range(2)]
                 if c == 3:
-                    frac = keep.tile([P, CHUNK, 4], F32, name="frac_last", tag="hold")
+                    frac = keep.tile([P, 2, CHUNK, 2], F32, name="frac_last", tag="hold")
                 else:
-                    frac = ring.tile([P, CHUNK, 4], F32, name="frac", bufs=3)
-                for e in range(2):
-                    nc.vector.tensor_scalar(turns[e][:], zs[e], 1.0 / TWO_PI, None, ALU.mult)
-                for e in range(2):
-                    nc.vector.scalar_tensor_tensor(
-                        frac[:, UNIT * e : UNIT * (e + 1), :], zs[e], 1.0 / TWO_PI, turns[e][:], ALU.mult, ALU.subtract
-                    )
-                hf[f, c] = ring.tile([P, CHUNK, 4], F32, name="hf", bufs=4)
-                nc.scalar.activation(hf[f, c][:], frac[:], ACT.Sin, scale=TWO_PI)
+                    frac = ring.tile([P, 2, CHUNK, 2], F32, name="frac", bufs=3)
+                for u in range(2):
+                    nc.vector.tensor_scalar(turns[u][:], zs[u], 1.0 / TWO_PI, None, ALU.mult)
+                for u in range(2):
+                    nc.vector.scalar_tensor_tensor(frac[:, u], zs[u], 1.0 / TWO_PI, turns[u][:], ALU.mult, ALU.subtract)
+                sines = ring.tile([P, CHUNK, 2, 2], F32, name="hf", bufs=4)
+                nc.scalar.activation(sines[:], frac[:].rearrange("p u n e -> p n u e"), ACT.Sin, scale=TWO_PI)
+                hf[f, c] = sines
             else:
                 if (f, c) == (1, 0):
-                    hf[f, c] = keep.tile([P, CHUNK, 4], F32, name="hf_first", tag="hold")
-                else:
-                    hf[f, c] = ring.tile([P, CHUNK, 4], F32, name="hf", bufs=4)
-                for e in range(2):
-                    nc.scalar.activation(
-                        hf[f, c][:, UNIT * e : UNIT * (e + 1), :], zs[e], ACT.Tanh if f == 1 else ACT.Exp
-                    )
+                    hf[f, 0] = keep.tile([P, 2, HALF, 2], F32, name="hf_first", tag="hold")
+                elif c % 2 == 0:
+                    hf[f, c // 2] = ring.tile([P, 2, HALF, 2], F32, name="hf_half", bufs=2)
+                c0 = CHUNK * (c % 2)
+                for u in range(2):
+                    nc.scalar.activation(hf[f, c // 2][:, u, c0 : c0 + CHUNK, :], zs[u], ACT.Tanh if f == 1 else ACT.Exp)
 
-        def apply_gain(f, c):
-            hb[f, c] = ring.tile([P, CHUNK, 4], BF16, name="hb", align_bytes=64)
-            engine = nc.gpsimd if f == 0 else nc.vector
-            engine.tensor_tensor(
-                hb[f, c][:], hf[f, c][:], gain_sb[:, f : f + 1, :].to_broadcast([P, CHUNK, 4]), ALU.mult
-            )
+        def apply_gain(f, j0, j1):
+            h, c0 = divmod(j0, HALF)
+            cols = slice(c0, c0 + j1 - j0)
+            if c0 == 0:
+                hb[f, h] = ring.tile([P, HALF, 2, 2], BF16, name="hb", align_bytes=64)
+            factor = gain_sb[:, f : f + 1].to_broadcast([P, j1 - j0, 2, 2])
+            if f == 0:
+                nc.gpsimd.tensor_tensor(hb[f, h][:, cols], hf[f, j0 // CHUNK][:], factor, ALU.mult)
+            else:
+                nc.vector.tensor_tensor(
+                    hb[f, h][:, cols], hf[f, h][:, :, cols, :].rearrange("p u n e -> p n u e"), factor, ALU.mult
+                )
 
-        def quantize_h(f, c):
-            h, c0 = divmod(c * CHUNK, HALF)
-            cols = slice(c0, c0 + CHUNK)
+        def quantize_h(f, j0, j1):
+            h, c0 = divmod(j0, HALF)
+            cols = slice(c0, c0 + j1 - j0)
             nc.vector.quantize_mx(
-                hq[f][h][:, cols].bitcast(FP8X4), hs[f][h][:, cols], hb[f, c][:].rearrange("p n t -> p (n t)")
+                hq[f][h][:, cols].bitcast(FP8X4), hs[f][h][:, cols], hb[f, h][:, cols].rearrange("p n u e -> p (n u e)")
             )
 
         ysb = [keep.tile([P, S], F32, name="ysb%d" % c) for c in range(4)]
@@ -210,49 +220,66 @@ def tile_list_nerve_loss_warning_kernel(
         cast_weight(0, 0, 0, nc.vector.tensor_copy)
         cast_weight(0, 0, 1, nc.scalar.copy)
         load_weight(1, 1)
-        quantize_weight(0, 0, 0)
-        quantize_weight(0, 0, 1)
+        quantize_weight(0, 0, 0, 2)
+        quantize_weight(0, 0, 2, 4)
         cast_weight(0, 1, 0, nc.vector.tensor_copy)
         cast_weight(0, 1, 1, nc.scalar.copy)
         load_weight(2, 0)
-        quantize_weight(0, 1, 0)
-        quantize_weight(0, 1, 1)
+        quantize_weight(0, 1, 0, 2)
+        quantize_weight(0, 1, 2, 4)
 
         order = [(f, c) for f in range(3) for c in range(4)]
         g2w = keep.tile([P, P2], U32, name="g2w", align_bytes=64)
         for i in range(len(order) + 2):
             if i < len(order):
                 features(*order[i])
+            if i == 4:
+                quantize_weight(2, 0, 0, 4)
+                nc.vector.tensor_copy(g2w[:], t2w[:].bitcast(U32).indirect(idx2[:]))
             if 1 <= i <= len(order):
-                apply_gain(*order[i - 1])
+                f, c = order[i - 1]
+                if (f, c) in ((1, 3), (2, 1)):
+                    apply_gain(f, CHUNK * (c - 1), CHUNK * (c + 1))
+                elif (f, c) not in ((1, 2), (2, 0)):
+                    apply_gain(f, CHUNK * c, CHUNK * (c + 1))
             if i >= 2:
-                quantize_h(*order[i - 2])
-            if i < 4:
-                f, a = 1 + i // 2, i % 2
+                f, c = order[i - 2]
+                if f == 2 and c >= 2:
+                    quantize_h(f, CHUNK * c, CHUNK * (c + 1))
+                elif c % 2 == 1:
+                    quantize_h(f, CHUNK * (c - 1), CHUNK * (c + 1))
+            if i == 0:
                 for u in range(2):
-                    cast_weight(f, a, u, nc.scalar.copy)
-                if i == 0:
-                    load_weight(2, 1)
-                if i == 1:
-                    t2w = placed([P, TB], I32, "t2w", slot[0])
-                    nc.sync.dma_start(t2w[:], tab2_words[0].rearrange("p t i -> p (t i)").bitcast(I32))
-                if i == 2:
-                    w5w = placed([P, N], I32, "w5w", slot[1])
-                    nc.sync.dma_start(w5w[:], w5_words[0].rearrange("p t i -> p (t i)").bitcast(I32))
-                if i == 3:
-                    w5s = placed([P, N], U8, "w5s", slot[2] + TB)
-                    ga_sb = placed([P, 4], F32, "ga_sb", slot[2] + TB + N)
-                    gb_sb = placed([P, 4], F32, "gb_sb", slot[2] + TB + N + 64)
-                    nc.gpsimd.memset(w5s[:].bitcast(I32), 0)
-                    with nc.allow_non_contiguous_dma(reason="one factor to a partition"):
-                        nc.sync.dma_start(ga_sb[:], ga.rearrange("(c p) -> p c", p=P))
-                        nc.sync.dma_start(gb_sb[:], gb.rearrange("(c p) -> p c", p=P))
-                    for q in range(4):
-                        nc.sync.dma_start(
-                            w5s[32 * q : 32 * q + 4, :].bitcast(I32), w5_scales[0, 4 * q : 4 * q + 4, :].bitcast(I32)
-                        )
+                    cast_weight(1, 0, u, None)
+                load_weight(2, 1)
+                quantize_weight(1, 0, 0, 4)
+            if i == 1:
                 for u in range(2):
-                    quantize_weight(f, a, u)
+                    cast_weight(1, 1, u, nc.scalar.copy)
+                t2w = placed([P, TB], I32, "t2w", slot[0])
+                nc.sync.dma_start(t2w[:], tab2_words[0].rearrange("p t i -> p (t i)").bitcast(I32))
+                quantize_weight(1, 1, 0, 4)
+            if i == 3:
+                for u in range(2):
+                    cast_weight(2, 0, u, nc.scalar.copy)
+                w5w = placed([P, N], I32, "w5w", slot[1])
+                nc.sync.dma_start(w5w[:], w5_words[0].rearrange("p t i -> p (t i)").bitcast(I32))
+            if i == 5:
+                for u in range(2):
+                    cast_weight(2, 1, u, nc.scalar.copy)
+                w5s = placed([P, N], U8, "w5s", slot[2] + TB)
+                ga_sb = placed([P, 4], F32, "ga_sb", slot[2] + TB + N)
+                gb_sb = placed([P, 4], F32, "gb_sb", slot[2] + TB + N + 64)
+                nc.gpsimd.memset(w5s[:].bitcast(I32), 0)
+                with nc.allow_non_contiguous_dma(reason="one factor to a partition"):
+                    nc.sync.dma_start(ga_sb[:], ga.rearrange("(c p) -> p c", p=P))
+                    nc.sync.dma_start(gb_sb[:], gb.rearrange("(c p) -> p c", p=P))
+                for q in range(4):
+                    nc.sync.dma_start(
+                        w5s[32 * q : 32 * q + 4, :].bitcast(I32), w5_scales[0, 4 * q : 4 * q + 4, :].bitcast(I32)
+                    )
+            if i == 6:
+                quantize_weight(2, 1, 0, 4)
             if i >= 2 and order[i - 2][1] == 1:
                 f = order[i - 2][0]
                 for c in range(4):
@@ -270,7 +297,6 @@ def tile_list_nerve_loss_warning_kernel(
                 copy_y(0, c)
             copy_y(1, c)
 
-        nc.vector.tensor_copy(g2w[:], t2w[:].bitcast(U32).indirect(idx2[:]))
         picked = []
         bbank = []
         for c in range(4):

@@ -3,8 +3,8 @@ from contextlib import ExitStack
 
 import concourse.mybir as mybir
 
-K, R, H, K2, N, T, S, TB, P2 = 1024, 512, 1536, 512, 512, 4096, 1024, 2048, 512
-FLOPS = 2 * (K * H * S + H * N * S + K2 * N * P2)
+K, R, H, K2, N, T, S, TB, PICKS = 1024, 512, 1536, 512, 512, 4096, 1024, 2048, 512
+FLOPS = 2 * (K * H * S + H * N * S + K2 * N * PICKS)
 
 F32 = mybir.dt.float32
 BF16 = mybir.dt.bfloat16
@@ -18,10 +18,11 @@ ACT = mybir.ActivationFunctionType
 ALU = mybir.AluOpType
 
 P = 128
-UNIT = 128
+PASS = 512
 CHUNK = 256
 HALF = 512
 SLOT = 8192
+SIN, TANH, EXP = 0, 1, 2
 TWO_PI = 2.0 * math.pi
 
 
@@ -32,67 +33,79 @@ def tile_list_nerve_loss_warning_kernel(
     nc = tc.nc
     with ExitStack() as ctx:
         keep = ctx.enter_context(tc.tile_pool(name="keep", bufs=1))
-        planes = ctx.enter_context(tc.tile_pool(name="planes", bufs=1))
+        shared = ctx.enter_context(tc.tile_pool(name="shared", bufs=1))
         ring = ctx.enter_context(tc.tile_pool(name="ring", bufs=3))
         zpool = ctx.enter_context(tc.psum_pool(name="zpool", bufs=4))
         ypool = ctx.enter_context(tc.psum_pool(name="ypool", bufs=1))
 
         idx = keep.tile([P, S // 16], U16, name="idx")
-        idx2 = keep.tile([P, P2 // 16], U16, name="idx2")
-        p1 = keep.tile([P, P2 // 16], U16, name="p1")
+        idx2 = keep.tile([P, PICKS // 16], U16, name="idx2")
+        p1 = keep.tile([P, PICKS // 16], U16, name="p1")
+
         def placed(shape, dtype, name, offset):
-            return planes.tile(shape, dtype, name=name, offset=offset, align_bytes=64)
+            return shared.tile(shape, dtype, name=name, offset=offset, align_bytes=64)
 
         slot = [8 * T, 8 * T + SLOT, 0]
-        tw = [placed([P, T], I32, "tw%d" % a, 4 * T * a) for a in range(2)]
-        ts = placed([P, T], U8, "ts", slot[1] - T // 2)
+        table = [placed([P, T], I32, "table%d" % a, 4 * T * a) for a in range(2)]
+        table_rows = placed([P, T], U8, "table_rows", slot[1] - T // 2)
         gain_sb = keep.tile([P, 3, 2, 2], F32, name="gain_sb")
-        gs_rows = keep.tile([P, S], U8, name="gs_rows")
-        gs = keep.tile([P, S], U8, name="gs", align_bytes=64)
+        picked_rows = keep.tile([P, S], U8, name="picked_rows")
+        v_scales = keep.tile([P, S], U8, name="v_scales", align_bytes=64)
 
         nc.sync.dma_start(idx[:], offs)
-        nc.sync.dma_start(ts[0:32, :].bitcast(I32), tab_scales.rearrange("a q t -> (a q) t").bitcast(I32))
+        nc.sync.dma_start(table_rows[0:32, :].bitcast(I32), tab_scales.rearrange("a q t -> (a q) t").bitcast(I32))
         nc.sync.dma_start(idx2[:], offs2)
         nc.sync.dma_start(p1[:], pos1)
         for a in range(2):
-            nc.sync.dma_start(tw[a][:], tab_words[a].rearrange("p t i -> p (t i)").bitcast(I32))
-        nc.sync.dma_start(gain_sb[:], gain.rearrange("(a p u e) -> p a u e", a=3, u=2, e=2))
+            nc.sync.dma_start(table[a][:], tab_words[a].rearrange("p t i -> p (t i)").bitcast(I32))
+        nc.sync.dma_start(gain_sb[:], gain.rearrange("(f p u e) -> p f u e", f=3, u=2, e=2))
 
-        t2s = keep.tile([P, TB], U8, name="t2s")
-        nc.gpsimd.memset(t2s[:].bitcast(I32), 0)
-        nc.vector.memset(ts[32:64, :].bitcast(I32), 0)
-        nc.vector.memset(ts[64:128, :].bitcast(I32), 0)
-        nc.vector.memset(gs[:].bitcast(I32), 0)
-        nc.vector.tensor_copy(gs_rows[:], ts[:].indirect(idx[:]))
+        table2_scales = keep.tile([P, TB], U8, name="table2_scales")
+        nc.gpsimd.memset(table2_scales[:].bitcast(I32), 0)
+        warm_in = keep.tile([P, 1], F32, name="warm_in")
+        warm_out = keep.tile([P, 1], F32, name="warm_out")
+        nc.vector.memset(warm_in[:], 0.0)
+        nc.scalar.activation(warm_out[:], warm_in[:], ACT.Silu)
+        nc.vector.memset(table_rows[32:64, :].bitcast(I32), 0)
+        nc.vector.memset(table_rows[64:128, :].bitcast(I32), 0)
+        nc.vector.memset(v_scales[:].bitcast(I32), 0)
+
+        nc.vector.tensor_copy(picked_rows[:], table_rows[:].indirect(idx[:]))
         for a, queue in enumerate((nc.scalar, nc.gpsimd)):
             for q in range(4):
                 queue.dma_start(
-                    gs[32 * q + 4 * a : 32 * q + 4 * a + 4, :].bitcast(I32),
-                    gs_rows[16 * a + 4 * q : 16 * a + 4 * q + 4, :].bitcast(I32),
+                    v_scales[32 * q + 4 * a : 32 * q + 4 * a + 4, :].bitcast(I32),
+                    picked_rows[16 * a + 4 * q : 16 * a + 4 * q + 4, :].bitcast(I32),
                 )
-
         for q in range(4):
-            nc.gpsimd.dma_start(t2s[32 * q : 32 * q + 4, :].bitcast(I32), tab2_scales[0, 4 * q : 4 * q + 4, :].bitcast(I32))
+            nc.gpsimd.dma_start(
+                table2_scales[32 * q : 32 * q + 4, :].bitcast(I32), tab2_scales[0, 4 * q : 4 * q + 4, :].bitcast(I32)
+            )
 
-        wraw = {}
+        w_raw = {}
 
         def load_weight(f, a):
             w = (w1, w2, w3)[f]
-            wraw[f, a] = placed([P, 4, R], F32, "wraw%d%d" % (f, a), slot[(2 * f + a) % 3])
-            nc.sync.dma_start(wraw[f, a][:], w[512 * a : 512 * (a + 1), :].rearrange("(p j) c -> p j c", j=4))
+            w_raw[f, a] = placed([P, 4, R], F32, "w_raw%d%d" % (f, a), slot[(2 * f + a) % 3])
+            nc.sync.dma_start(w_raw[f, a][:], w[PASS * a : PASS * (a + 1), :].rearrange("(p j) c -> p j c", j=4))
 
-        load_weight(0, 0)
-        load_weight(0, 1)
+        load_weight(SIN, 0)
+        load_weight(SIN, 1)
 
-        gw = [[keep.tile([P, HALF], U32, name="gw%d%d" % (a, h), align_bytes=64) for h in range(2)] for a in range(2)]
+        v_words = [
+            [keep.tile([P, HALF], U32, name="v_words%d%d" % (a, h), align_bytes=64) for h in range(2)] for a in range(2)
+        ]
+        list_cols = HALF // 16
         for a in range(2):
             for h in range(2):
-                nc.vector.tensor_copy(gw[a][h][:], tw[a][:].bitcast(U32).indirect(idx[:, 32 * h : 32 * (h + 1)]))
+                nc.vector.tensor_copy(
+                    v_words[a][h][:], table[a][:].bitcast(U32).indirect(idx[:, list_cols * h : list_cols * (h + 1)])
+                )
             if a == 0:
-                g2s = placed([P, P2], U8, "g2s", SLOT + 8 * N)
-                nc.vector.tensor_copy(g2s[:], t2s[:].indirect(idx2[:]))
+                v2_scales = placed([P, PICKS], U8, "v2_scales", SLOT + 8 * N)
+                nc.vector.tensor_copy(v2_scales[:], table2_scales[:].indirect(idx2[:]))
 
-        load_weight(1, 0)
+        load_weight(TANH, 0)
         w4w = placed([P, 3, 2 * N], U8, "w4w", SLOT)
         nc.sync.dma_start(w4w[:].bitcast(I32), w4_words.rearrange("a p n -> p a n").bitcast(I32))
         w4s = placed([P, 3, N], U8, "w4s", 4 * T)
@@ -103,32 +116,40 @@ def tile_list_nerve_loss_warning_kernel(
                 w4_scales[:, 4 * q : 4 * q + 4, :].rearrange("a r n -> r a n").bitcast(I32),
             )
 
-        wq = [[keep.tile([P, R], U32, name="wq%d%d" % (f, a), align_bytes=64) for a in range(2)] for f in range(3)]
-        wsc = [[keep.tile([P, R], U8, name="wsc%d%d" % (f, a), align_bytes=64) for a in range(2)] for f in range(3)]
-        wb = {}
+        w_codes = [[keep.tile([P, R], U32, name="w_codes%d%d" % (f, a), align_bytes=64) for a in range(2)] for f in range(3)]
+        w_scales = [[keep.tile([P, R], U8, name="w_scales%d%d" % (f, a), align_bytes=64) for a in range(2)] for f in range(3)]
+        w_bf16 = {}
 
-        def cast_weight(f, a, u, copy):
+        def rounding_views(f, a, u):
             if u == 0:
-                wb[f, a] = ring.tile([P, 4, 128, 4], BF16, name="wb", align_bytes=64, bufs=3)
-            dst = wb[f, a][:, 2 * u : 2 * u + 2]
-            src = wraw[f, a][:].rearrange("p j (m t) -> p j m t", t=4)[:, :, :, 2 * u : 2 * u + 2]
-            if copy is None:
-                nc.gpsimd.tensor_scalar(
-                    dst.rearrange("p t m j -> p m t j"), src.rearrange("p j m t -> p m t j"), 1.0, 0.0, ALU.mult, ALU.add
-                )
-            else:
-                copy(dst.rearrange("p t m j -> p m j t"), src.rearrange("p j m t -> p m j t"))
+                w_bf16[f, a] = ring.tile([P, 4, P, 4], BF16, name="w_bf16", align_bytes=64)
+            dst = w_bf16[f, a][:, 2 * u : 2 * u + 2]
+            src = w_raw[f, a][:].rearrange("p j (m t) -> p j m t", t=4)[:, :, :, 2 * u : 2 * u + 2]
+            return dst, src
 
-        def quantize_weight(f, a, t0, t1):
-            cols = slice(128 * t0, 128 * t1)
-            nc.vector.quantize_mx(
-                wq[f][a][:, cols].bitcast(FP8X4), wsc[f][a][:, cols], wb[f, a][:, t0:t1].rearrange("p t m j -> p (t m j)")
+        def round_weight(f, a, u, copy):
+            dst, src = rounding_views(f, a, u)
+            copy(dst.rearrange("p t m j -> p m j t"), src.rearrange("p j m t -> p m j t"))
+
+        def round_weight_on_gpsimd(f, a, u):
+            dst, src = rounding_views(f, a, u)
+            nc.gpsimd.tensor_scalar(
+                dst.rearrange("p t m j -> p m t j"), src.rearrange("p j m t -> p m t j"), 1.0, 0.0, ALU.mult, ALU.add
             )
 
-        hq = [[keep.tile([P, HALF], U32, name="hq%d%d" % (f, h), align_bytes=64) for h in range(2)] for f in range(3)]
-        hs = [[keep.tile([P, HALF], U8, name="hs%d%d" % (f, h), align_bytes=64) for h in range(2)] for f in range(3)]
-        hf = {}
-        hb = {}
+        def quantize_weight(f, a, t0, t1):
+            cols = slice(P * t0, P * t1)
+            nc.vector.quantize_mx(
+                w_codes[f][a][:, cols].bitcast(FP8X4),
+                w_scales[f][a][:, cols],
+                w_bf16[f, a][:, t0:t1].rearrange("p t m j -> p (t m j)"),
+            )
+
+        h_codes = [[keep.tile([P, HALF], U32, name="h_codes%d%d" % (f, h), align_bytes=64) for h in range(2)] for f in range(3)]
+        h_scales = [[keep.tile([P, HALF], U8, name="h_scales%d%d" % (f, h), align_bytes=64) for h in range(2)] for f in range(3)]
+        sines = {}
+        values = {}
+        h_bf16 = {}
 
         def first_product(f, c, u):
             z = zpool.tile([P, 2, CHUNK], F32, name="z")
@@ -138,10 +159,10 @@ def tile_list_nerve_loss_warning_kernel(
                     t = 2 * u + e
                     nc.tensor.matmul_mx(
                         z[:, e, :],
-                        lhsT=wq[f][a][:, 128 * t : 128 * (t + 1)].bitcast(FP8X4),
-                        lhsT_scale=wsc[f][a][:, 128 * t : 128 * (t + 1)],
-                        rhs=gw[a][h][:, c0 : c0 + CHUNK].bitcast(FP8X4),
-                        rhs_scale=gs[4 * a : P, c * CHUNK : (c + 1) * CHUNK],
+                        lhsT=w_codes[f][a][:, P * t : P * (t + 1)].bitcast(FP8X4),
+                        lhsT_scale=w_scales[f][a][:, P * t : P * (t + 1)],
+                        rhs=v_words[a][h][:, c0 : c0 + CHUNK].bitcast(FP8X4),
+                        rhs_scale=v_scales[4 * a : P, c * CHUNK : (c + 1) * CHUNK],
                         start=(a == 0 and e == 0),
                         stop=(a == 1 and e == 1),
                     )
@@ -149,179 +170,172 @@ def tile_list_nerve_loss_warning_kernel(
 
         def features(f, c):
             zs = [first_product(f, c, u) for u in range(2)]
-            if f == 0:
+            if f == SIN:
                 turns = [ring.tile([P, CHUNK, 2], I32, name="turns", bufs=4) for u in range(2)]
-                if c == 3:
-                    frac = keep.tile([P, 2, CHUNK, 2], F32, name="frac_last", tag="hold")
-                else:
-                    frac = ring.tile([P, 2, CHUNK, 2], F32, name="frac", bufs=3)
+                rest = ring.tile([P, 2, CHUNK, 2], F32, name="rest")
                 for u in range(2):
                     nc.vector.tensor_scalar(turns[u][:], zs[u], 1.0 / TWO_PI, None, ALU.mult)
                 for u in range(2):
-                    nc.vector.scalar_tensor_tensor(frac[:, u], zs[u], 1.0 / TWO_PI, turns[u][:], ALU.mult, ALU.subtract)
-                sines = ring.tile([P, CHUNK, 2, 2], F32, name="hf", bufs=4)
-                nc.scalar.activation(sines[:], frac[:].rearrange("p u n e -> p n u e"), ACT.Sin, scale=TWO_PI)
-                hf[f, c] = sines
+                    nc.vector.scalar_tensor_tensor(rest[:, u], zs[u], 1.0 / TWO_PI, turns[u][:], ALU.mult, ALU.subtract)
+                sines[c] = ring.tile([P, CHUNK, 2, 2], F32, name="sines", bufs=4)
+                nc.scalar.activation(sines[c][:], rest[:].rearrange("p u n e -> p n u e"), ACT.Sin, scale=TWO_PI)
             else:
-                if (f, c) == (1, 0):
-                    hf[f, 0] = keep.tile([P, 2, HALF, 2], F32, name="hf_first", tag="hold")
-                elif c % 2 == 0:
-                    hf[f, c // 2] = ring.tile([P, 2, HALF, 2], F32, name="hf_half", bufs=2)
-                c0 = CHUNK * (c % 2)
+                h, c0 = divmod(c * CHUNK, HALF)
+                if c0 == 0:
+                    values[f, h] = ring.tile([P, 2, HALF, 2], F32, name="values")
                 for u in range(2):
-                    nc.scalar.activation(hf[f, c // 2][:, u, c0 : c0 + CHUNK, :], zs[u], ACT.Tanh if f == 1 else ACT.Exp)
+                    nc.scalar.activation(
+                        values[f, h][:, u, c0 : c0 + CHUNK, :], zs[u], ACT.Tanh if f == TANH else ACT.Exp
+                    )
 
-        def apply_gain(f, j0, j1):
-            h, c0 = divmod(j0, HALF)
-            cols = slice(c0, c0 + j1 - j0)
+        def apply_gain(f, c):
+            h, c0 = divmod(c * CHUNK, HALF)
+            cols = slice(c0, c0 + CHUNK)
             if c0 == 0:
-                hb[f, h] = ring.tile([P, HALF, 2, 2], BF16, name="hb", align_bytes=64)
-            factor = gain_sb[:, f : f + 1].to_broadcast([P, j1 - j0, 2, 2])
-            if f == 0:
-                nc.gpsimd.tensor_tensor(hb[f, h][:, cols], hf[f, j0 // CHUNK][:], factor, ALU.mult)
+                h_bf16[f, h] = ring.tile([P, HALF, 2, 2], BF16, name="h_bf16", align_bytes=64)
+            dst = h_bf16[f, h][:, cols]
+            factor = gain_sb[:, f : f + 1].to_broadcast([P, CHUNK, 2, 2])
+            if f != SIN:
+                nc.vector.tensor_tensor(dst, values[f, h][:, :, cols, :].rearrange("p u n e -> p n u e"), factor, ALU.mult)
+            elif c == S // CHUNK - 1:
+                nc.vector.tensor_tensor(dst, sines[c][:], factor, ALU.mult)
             else:
-                nc.vector.tensor_tensor(
-                    hb[f, h][:, cols], hf[f, h][:, :, cols, :].rearrange("p u n e -> p n u e"), factor, ALU.mult
-                )
+                for n0 in (0, CHUNK // 2):
+                    piece = slice(n0, n0 + CHUNK // 2)
+                    nc.gpsimd.tensor_tensor(dst[:, piece], sines[c][:, piece], factor[:, piece], ALU.mult)
 
         def quantize_h(f, j0, j1):
             h, c0 = divmod(j0, HALF)
             cols = slice(c0, c0 + j1 - j0)
             nc.vector.quantize_mx(
-                hq[f][h][:, cols].bitcast(FP8X4), hs[f][h][:, cols], hb[f, h][:, cols].rearrange("p n u e -> p (n u e)")
+                h_codes[f][h][:, cols].bitcast(FP8X4),
+                h_scales[f][h][:, cols],
+                h_bf16[f, h][:, cols].rearrange("p n u e -> p (n u e)"),
             )
 
-        ysb = [keep.tile([P, S], F32, name="ysb%d" % c) for c in range(4)]
-        ybank = {}
+        y_sb = [keep.tile([P, S], F32, name="y_sb%d" % g) for g in range(4)]
+        y_bank = {}
 
-        def second_pass(h, c, f, cols, start, stop):
-            if start:
-                if h == 0:
-                    ybank[h, c] = ypool.tile([P, HALF], F32, name="y%d" % c)
-                else:
-                    ybank[h, c] = zpool.tile([P, HALF], F32, name="z")
+        def second_pass(h, g, f, cols, start, stop):
+            if start and h == 0:
+                y_bank[h, g] = ypool.tile([P, HALF], F32, name="y%d" % g)
+            elif start:
+                y_bank[h, g] = zpool.tile([P, HALF], F32, name="z")
             nc.tensor.matmul_mx(
-                ybank[h, c][:, cols],
-                lhsT=w4w[:, f, 256 * c : 256 * (c + 1)].bitcast(FP4X4),
-                lhsT_scale=w4s[:, f, 128 * c : 128 * (c + 1)],
-                rhs=hq[f][h][:, cols].bitcast(FP8X4),
-                rhs_scale=hs[f][h][:, cols],
+                y_bank[h, g][:, cols],
+                lhsT=w4w[:, f, 2 * P * g : 2 * P * (g + 1)].bitcast(FP4X4),
+                lhsT_scale=w4s[:, f, P * g : P * (g + 1)],
+                rhs=h_codes[f][h][:, cols].bitcast(FP8X4),
+                rhs_scale=h_scales[f][h][:, cols],
                 start=start,
                 stop=stop,
             )
 
-        def copy_y(h, c):
+        def copy_y(h, g):
             nc.scalar.activation(
-                ysb[c][:, HALF * h : HALF * (h + 1)], ybank[h, c][:], ACT.Copy, scale=ga_sb[:, c : c + 1]
+                y_sb[g][:, HALF * h : HALF * (h + 1)], y_bank[h, g][:], ACT.Copy, scale=ga_sb[:, g : g + 1]
             )
 
+        for a in range(2):
+            round_weight(SIN, a, 0, nc.vector.tensor_copy)
+            round_weight(SIN, a, 1, nc.scalar.copy)
+            load_weight(*divmod(3 + a, 2))
+            quantize_weight(SIN, a, 0, 2)
+            quantize_weight(SIN, a, 2, 4)
+
+        chunks = [(f, c) for f in range(3) for c in range(S // CHUNK)]
+        steps = len(chunks)
         whole = slice(0, HALF)
+        v2_words = keep.tile([P, PICKS], U32, name="v2_words", align_bytes=64)
+        for i in range(steps + 2):
+            if i < steps:
+                features(*chunks[i])
+            if 1 <= i <= steps:
+                apply_gain(*chunks[i - 1])
+            if i >= steps:
+                f, c = chunks[i - 2]
+                quantize_h(f, CHUNK * c, CHUNK * (c + 1))
+            elif i >= 2 and i % 2 == 1:
+                f, c = chunks[i - 2]
+                quantize_h(f, CHUNK * (c - 1), CHUNK * (c + 1))
 
-        cast_weight(0, 0, 0, nc.vector.tensor_copy)
-        cast_weight(0, 0, 1, nc.scalar.copy)
-        load_weight(1, 1)
-        quantize_weight(0, 0, 0, 2)
-        quantize_weight(0, 0, 2, 4)
-        cast_weight(0, 1, 0, nc.vector.tensor_copy)
-        cast_weight(0, 1, 1, nc.scalar.copy)
-        load_weight(2, 0)
-        quantize_weight(0, 1, 0, 2)
-        quantize_weight(0, 1, 2, 4)
-
-        order = [(f, c) for f in range(3) for c in range(4)]
-        g2w = keep.tile([P, P2], U32, name="g2w", align_bytes=64)
-        for i in range(len(order) + 2):
-            if i < len(order):
-                features(*order[i])
-            if i == 4:
-                quantize_weight(2, 0, 0, 4)
-                nc.vector.tensor_copy(g2w[:], t2w[:].bitcast(U32).indirect(idx2[:]))
-            if 1 <= i <= len(order):
-                f, c = order[i - 1]
-                if (f, c) in ((1, 3), (2, 1)):
-                    apply_gain(f, CHUNK * (c - 1), CHUNK * (c + 1))
-                elif (f, c) not in ((1, 2), (2, 0)):
-                    apply_gain(f, CHUNK * c, CHUNK * (c + 1))
-            if i >= 2:
-                f, c = order[i - 2]
-                if f == 2 and c >= 2:
-                    quantize_h(f, CHUNK * c, CHUNK * (c + 1))
-                elif c % 2 == 1:
-                    quantize_h(f, CHUNK * (c - 1), CHUNK * (c + 1))
             if i == 0:
                 for u in range(2):
-                    cast_weight(1, 0, u, None)
-                load_weight(2, 1)
-                quantize_weight(1, 0, 0, 4)
+                    round_weight_on_gpsimd(TANH, 0, u)
+                load_weight(EXP, 1)
+                quantize_weight(TANH, 0, 0, 4)
             if i == 1:
                 for u in range(2):
-                    cast_weight(1, 1, u, nc.scalar.copy)
-                t2w = placed([P, TB], I32, "t2w", slot[0])
-                nc.sync.dma_start(t2w[:], tab2_words[0].rearrange("p t i -> p (t i)").bitcast(I32))
-                quantize_weight(1, 1, 0, 4)
-            if i == 3:
+                    round_weight(TANH, 1, u, nc.scalar.copy)
+                table2 = placed([P, TB], I32, "table2", slot[0])
+                nc.sync.dma_start(table2[:], tab2_words[0].rearrange("p t i -> p (t i)").bitcast(I32))
+                quantize_weight(TANH, 1, 0, 4)
+            if i == 2:
                 for u in range(2):
-                    cast_weight(2, 0, u, nc.scalar.copy)
+                    round_weight(EXP, 0, u, nc.scalar.copy)
                 w5w = placed([P, N], I32, "w5w", slot[1])
                 nc.sync.dma_start(w5w[:], w5_words[0].rearrange("p t i -> p (t i)").bitcast(I32))
-            if i == 5:
+            if i == 4:
                 for u in range(2):
-                    cast_weight(2, 1, u, nc.scalar.copy)
+                    round_weight(EXP, 1, u, nc.scalar.copy)
                 w5s = placed([P, N], U8, "w5s", slot[2] + TB)
                 ga_sb = placed([P, 4], F32, "ga_sb", slot[2] + TB + N)
                 gb_sb = placed([P, 4], F32, "gb_sb", slot[2] + TB + N + 64)
                 nc.gpsimd.memset(w5s[:].bitcast(I32), 0)
-                with nc.allow_non_contiguous_dma(reason="one factor to a partition"):
-                    nc.sync.dma_start(ga_sb[:], ga.rearrange("(c p) -> p c", p=P))
-                    nc.sync.dma_start(gb_sb[:], gb.rearrange("(c p) -> p c", p=P))
+                with nc.allow_non_contiguous_dma(reason="one factor for each output row, a row to a partition"):
+                    nc.sync.dma_start(ga_sb[:], ga.rearrange("(g p) -> p g", p=P))
+                    nc.sync.dma_start(gb_sb[:], gb.rearrange("(g p) -> p g", p=P))
                 for q in range(4):
                     nc.sync.dma_start(
                         w5s[32 * q : 32 * q + 4, :].bitcast(I32), w5_scales[0, 4 * q : 4 * q + 4, :].bitcast(I32)
                     )
-            if i == 6:
-                quantize_weight(2, 1, 0, 4)
-            if i >= 2 and order[i - 2][1] == 1:
-                f = order[i - 2][0]
-                for c in range(4):
-                    second_pass(0, c, f, whole, f == 0, f == 2)
-            if i == 11:
-                copy_y(0, 0)
-            if i == 12:
-                for c in range(4):
-                    second_pass(1, c, 0, whole, True, False)
-                    second_pass(1, c, 1, whole, False, False)
-                    second_pass(1, c, 2, slice(0, CHUNK), False, False)
-        for c in range(4):
-            second_pass(1, c, 2, slice(CHUNK, HALF), False, True)
-            if c > 0:
-                copy_y(0, c)
-            copy_y(1, c)
+            if i in (5, 6):
+                quantize_weight(EXP, i - 5, 0, 4)
 
-        picked = []
-        bbank = []
-        for c in range(4):
-            b = ypool.tile([P, P2], F32, name="y%d" % c)
+            if i >= 2 and chunks[i - 2][1] == 1:
+                f = chunks[i - 2][0]
+                for g in range(4):
+                    second_pass(0, g, f, whole, f == SIN, f == EXP)
+                if f == EXP:
+                    copy_y(0, 0)
+            if i == steps:
+                for g in range(4):
+                    second_pass(1, g, SIN, whole, True, False)
+                    second_pass(1, g, TANH, whole, False, False)
+                    second_pass(1, g, EXP, slice(0, CHUNK), False, False)
+        for g in range(4):
+            second_pass(1, g, EXP, slice(CHUNK, HALF), False, True)
+            if g > 0:
+                copy_y(0, g)
+            copy_y(1, g)
+
+        nc.vector.tensor_copy(v2_words[:], table2[:].bitcast(U32).indirect(idx2[:]))
+        b_bank = []
+        for g in range(4):
+            b = ypool.tile([P, PICKS], F32, name="y%d" % g)
             nc.tensor.matmul_mx(
                 b[:],
-                lhsT=w5w[:, 128 * c : 128 * (c + 1)].bitcast(FP8X4),
-                lhsT_scale=w5s[:, 128 * c : 128 * (c + 1)],
-                rhs=g2w[:].bitcast(FP8X4),
-                rhs_scale=g2s[:],
+                lhsT=w5w[:, P * g : P * (g + 1)].bitcast(FP8X4),
+                lhsT_scale=w5s[:, P * g : P * (g + 1)],
+                rhs=v2_words[:].bitcast(FP8X4),
+                rhs_scale=v2_scales[:],
                 start=True,
                 stop=True,
             )
-            bbank.append(b)
-        pieces = [(0, 0, P2), (1, 0, P2), (2, 0, P2), (3, 0, P2 // 2), (3, P2 // 2, P2)]
+            b_bank.append(b)
+
+        pieces = [(g, 0, PICKS) for g in range(3)] + [(3, 0, PICKS // 2), (3, PICKS // 2, PICKS)]
+        picked = []
         for i in range(len(pieces) + 1):
             if i < len(pieces):
-                c, j0, j1 = pieces[i]
-                pk = ring.tile([P, j1 - j0], F32, name="pk")
-                nc.vector.tensor_copy(pk[:], ysb[c][:].indirect(p1[:, j0 // 16 : j1 // 16]))
-                picked.append(pk)
+                g, j0, j1 = pieces[i]
+                y_picked = ring.tile([P, j1 - j0], F32, name="y_picked")
+                nc.vector.tensor_copy(y_picked[:], y_sb[g][:].indirect(p1[:, j0 // 16 : j1 // 16]))
+                picked.append(y_picked)
             if i >= 1:
-                c, j0, j1 = pieces[i - 1]
-                res = keep.tile([P, j1 - j0], F32, name="res%d" % (i - 1))
+                g, j0, j1 = pieces[i - 1]
+                result = keep.tile([P, j1 - j0], F32, name="result%d" % (i - 1))
                 nc.vector.scalar_tensor_tensor(
-                    res[:], bbank[c][:, j0:j1], gb_sb[:, c : c + 1], picked[i - 1][:], ALU.mult, ALU.max
+                    result[:], b_bank[g][:, j0:j1], gb_sb[:, g : g + 1], picked[i - 1][:], ALU.mult, ALU.max
                 )
-                nc.sync.dma_start(out[128 * c : 128 * (c + 1), j0:j1], res[:])
+                nc.sync.dma_start(out[P * g : P * (g + 1), j0:j1], result[:])

import math
from contextlib import ExitStack

import concourse.mybir as mybir

K, R, H, K2, N, T, S, TB, PICKS = 1024, 512, 1536, 512, 512, 4096, 1024, 2048, 512
FLOPS = 2 * (K * H * S + H * N * S + K2 * N * PICKS)

F32 = mybir.dt.float32
BF16 = mybir.dt.bfloat16
I32 = mybir.dt.int32
U32 = mybir.dt.uint32
U16 = mybir.dt.uint16
U8 = mybir.dt.uint8
FP8X4 = mybir.dt.float8_e4m3fn_x4
FP4X4 = mybir.dt.float4_e2m1fn_x4
ACT = mybir.ActivationFunctionType
ALU = mybir.AluOpType

P = 128
PASS = 512
CHUNK = 256
HALF = 512
SLOT = 8192
SIN, TANH, EXP = 0, 1, 2
TWO_PI = 2.0 * math.pi


def tile_list_nerve_loss_warning_kernel(
    tc, tab_words, tab_scales, offs, tab2_words, tab2_scales, offs2, pos1,
    w1, w2, w3, gain, w4_words, w4_scales, w5_words, w5_scales, ga, gb, out,
):
    nc = tc.nc
    with ExitStack() as ctx:
        keep = ctx.enter_context(tc.tile_pool(name="keep", bufs=1))
        shared = ctx.enter_context(tc.tile_pool(name="shared", bufs=1))
        ring = ctx.enter_context(tc.tile_pool(name="ring", bufs=3))
        zpool = ctx.enter_context(tc.psum_pool(name="zpool", bufs=4))
        ypool = ctx.enter_context(tc.psum_pool(name="ypool", bufs=1))

        idx = keep.tile([P, S // 16], U16, name="idx")
        idx2 = keep.tile([P, PICKS // 16], U16, name="idx2")
        p1 = keep.tile([P, PICKS // 16], U16, name="p1")

        def placed(shape, dtype, name, offset):
            return shared.tile(shape, dtype, name=name, offset=offset, align_bytes=64)

        slot = [8 * T, 8 * T + SLOT, 0]
        table = [placed([P, T], I32, "table%d" % a, 4 * T * a) for a in range(2)]
        table_rows = placed([P, T], U8, "table_rows", slot[1] - T // 2)
        gain_sb = keep.tile([P, 3, 2, 2], F32, name="gain_sb")
        picked_rows = keep.tile([P, S], U8, name="picked_rows")
        v_scales = keep.tile([P, S], U8, name="v_scales", align_bytes=64)

        nc.sync.dma_start(idx[:], offs)
        nc.sync.dma_start(table_rows[0:32, :].bitcast(I32), tab_scales.rearrange("a q t -> (a q) t").bitcast(I32))
        nc.sync.dma_start(idx2[:], offs2)
        nc.sync.dma_start(p1[:], pos1)
        for a in range(2):
            nc.sync.dma_start(table[a][:], tab_words[a].rearrange("p t i -> p (t i)").bitcast(I32))
        nc.sync.dma_start(gain_sb[:], gain.rearrange("(f p u e) -> p f u e", f=3, u=2, e=2))

        table2_scales = keep.tile([P, TB], U8, name="table2_scales")
        nc.gpsimd.memset(table2_scales[:].bitcast(I32), 0)
        warm_in = keep.tile([P, 1], F32, name="warm_in")
        warm_out = keep.tile([P, 1], F32, name="warm_out")
        nc.vector.memset(warm_in[:], 0.0)
        nc.scalar.activation(warm_out[:], warm_in[:], ACT.Silu)
        nc.vector.memset(table_rows[32:64, :].bitcast(I32), 0)
        nc.vector.memset(table_rows[64:128, :].bitcast(I32), 0)
        nc.vector.memset(v_scales[:].bitcast(I32), 0)

        nc.vector.tensor_copy(picked_rows[:], table_rows[:].indirect(idx[:]))
        for a, queue in enumerate((nc.scalar, nc.gpsimd)):
            for q in range(4):
                queue.dma_start(
                    v_scales[32 * q + 4 * a : 32 * q + 4 * a + 4, :].bitcast(I32),
                    picked_rows[16 * a + 4 * q : 16 * a + 4 * q + 4, :].bitcast(I32),
                )
        for q in range(4):
            nc.gpsimd.dma_start(
                table2_scales[32 * q : 32 * q + 4, :].bitcast(I32), tab2_scales[0, 4 * q : 4 * q + 4, :].bitcast(I32)
            )

        w_raw = {}

        def load_weight(f, a):
            w = (w1, w2, w3)[f]
            w_raw[f, a] = placed([P, 4, R], F32, "w_raw%d%d" % (f, a), slot[(2 * f + a) % 3])
            nc.sync.dma_start(w_raw[f, a][:], w[PASS * a : PASS * (a + 1), :].rearrange("(p j) c -> p j c", j=4))

        load_weight(SIN, 0)
        load_weight(SIN, 1)

        v_words = [
            [keep.tile([P, HALF], U32, name="v_words%d%d" % (a, h), align_bytes=64) for h in range(2)] for a in range(2)
        ]
        list_cols = HALF // 16
        for a in range(2):
            for h in range(2):
                nc.vector.tensor_copy(
                    v_words[a][h][:], table[a][:].bitcast(U32).indirect(idx[:, list_cols * h : list_cols * (h + 1)])
                )
            if a == 0:
                v2_scales = placed([P, PICKS], U8, "v2_scales", SLOT + 8 * N)
                nc.vector.tensor_copy(v2_scales[:], table2_scales[:].indirect(idx2[:]))

        load_weight(TANH, 0)
        w4w = placed([P, 3, 2 * N], U8, "w4w", SLOT)
        nc.sync.dma_start(w4w[:].bitcast(I32), w4_words.rearrange("a p n -> p a n").bitcast(I32))
        w4s = placed([P, 3, N], U8, "w4s", 4 * T)
        nc.gpsimd.memset(w4s[:].bitcast(I32), 0)
        for q in range(4):
            nc.sync.dma_start(
                w4s[32 * q : 32 * q + 4, :, :].bitcast(I32),
                w4_scales[:, 4 * q : 4 * q + 4, :].rearrange("a r n -> r a n").bitcast(I32),
            )

        w_codes = [[keep.tile([P, R], U32, name="w_codes%d%d" % (f, a), align_bytes=64) for a in range(2)] for f in range(3)]
        w_scales = [[keep.tile([P, R], U8, name="w_scales%d%d" % (f, a), align_bytes=64) for a in range(2)] for f in range(3)]
        w_bf16 = {}

        def rounding_views(f, a, u):
            if u == 0:
                w_bf16[f, a] = ring.tile([P, 4, P, 4], BF16, name="w_bf16", align_bytes=64)
            dst = w_bf16[f, a][:, 2 * u : 2 * u + 2]
            src = w_raw[f, a][:].rearrange("p j (m t) -> p j m t", t=4)[:, :, :, 2 * u : 2 * u + 2]
            return dst, src

        def round_weight(f, a, u, copy):
            dst, src = rounding_views(f, a, u)
            copy(dst.rearrange("p t m j -> p m j t"), src.rearrange("p j m t -> p m j t"))

        def round_weight_on_gpsimd(f, a, u):
            dst, src = rounding_views(f, a, u)
            nc.gpsimd.tensor_scalar(
                dst.rearrange("p t m j -> p m t j"), src.rearrange("p j m t -> p m t j"), 1.0, 0.0, ALU.mult, ALU.add
            )

        def quantize_weight(f, a, t0, t1):
            cols = slice(P * t0, P * t1)
            nc.vector.quantize_mx(
                w_codes[f][a][:, cols].bitcast(FP8X4),
                w_scales[f][a][:, cols],
                w_bf16[f, a][:, t0:t1].rearrange("p t m j -> p (t m j)"),
            )

        h_codes = [[keep.tile([P, HALF], U32, name="h_codes%d%d" % (f, h), align_bytes=64) for h in range(2)] for f in range(3)]
        h_scales = [[keep.tile([P, HALF], U8, name="h_scales%d%d" % (f, h), align_bytes=64) for h in range(2)] for f in range(3)]
        sines = {}
        values = {}
        h_bf16 = {}

        def first_product(f, c, u):
            z = zpool.tile([P, 2, CHUNK], F32, name="z")
            h, c0 = divmod(c * CHUNK, HALF)
            for a in range(2):
                for e in range(2):
                    t = 2 * u + e
                    nc.tensor.matmul_mx(
                        z[:, e, :],
                        lhsT=w_codes[f][a][:, P * t : P * (t + 1)].bitcast(FP8X4),
                        lhsT_scale=w_scales[f][a][:, P * t : P * (t + 1)],
                        rhs=v_words[a][h][:, c0 : c0 + CHUNK].bitcast(FP8X4),
                        rhs_scale=v_scales[4 * a : P, c * CHUNK : (c + 1) * CHUNK],
                        start=(a == 0 and e == 0),
                        stop=(a == 1 and e == 1),
                    )
            return z[:].rearrange("p e n -> p n e")

        def features(f, c):
            zs = [first_product(f, c, u) for u in range(2)]
            if f == SIN:
                turns = [ring.tile([P, CHUNK, 2], I32, name="turns", bufs=4) for u in range(2)]
                rest = ring.tile([P, 2, CHUNK, 2], F32, name="rest")
                for u in range(2):
                    nc.vector.tensor_scalar(turns[u][:], zs[u], 1.0 / TWO_PI, None, ALU.mult)
                for u in range(2):
                    nc.vector.scalar_tensor_tensor(rest[:, u], zs[u], 1.0 / TWO_PI, turns[u][:], ALU.mult, ALU.subtract)
                sines[c] = ring.tile([P, CHUNK, 2, 2], F32, name="sines", bufs=4)
                nc.scalar.activation(sines[c][:], rest[:].rearrange("p u n e -> p n u e"), ACT.Sin, scale=TWO_PI)
            else:
                h, c0 = divmod(c * CHUNK, HALF)
                if c0 == 0:
                    values[f, h] = ring.tile([P, 2, HALF, 2], F32, name="values")
                for u in range(2):
                    nc.scalar.activation(
                        values[f, h][:, u, c0 : c0 + CHUNK, :], zs[u], ACT.Tanh if f == TANH else ACT.Exp
                    )

        def apply_gain(f, c):
            h, c0 = divmod(c * CHUNK, HALF)
            cols = slice(c0, c0 + CHUNK)
            if c0 == 0:
                h_bf16[f, h] = ring.tile([P, HALF, 2, 2], BF16, name="h_bf16", align_bytes=64)
            dst = h_bf16[f, h][:, cols]
            factor = gain_sb[:, f : f + 1].to_broadcast([P, CHUNK, 2, 2])
            if f != SIN:
                nc.vector.tensor_tensor(dst, values[f, h][:, :, cols, :].rearrange("p u n e -> p n u e"), factor, ALU.mult)
            elif c == S // CHUNK - 1:
                nc.vector.tensor_tensor(dst, sines[c][:], factor, ALU.mult)
            else:
                for n0 in (0, CHUNK // 2):
                    piece = slice(n0, n0 + CHUNK // 2)
                    nc.gpsimd.tensor_tensor(dst[:, piece], sines[c][:, piece], factor[:, piece], ALU.mult)

        def quantize_h(f, j0, j1):
            h, c0 = divmod(j0, HALF)
            cols = slice(c0, c0 + j1 - j0)
            nc.vector.quantize_mx(
                h_codes[f][h][:, cols].bitcast(FP8X4),
                h_scales[f][h][:, cols],
                h_bf16[f, h][:, cols].rearrange("p n u e -> p (n u e)"),
            )

        y_sb = [keep.tile([P, S], F32, name="y_sb%d" % g) for g in range(4)]
        y_bank = {}

        def second_pass(h, g, f, cols, start, stop):
            if start and h == 0:
                y_bank[h, g] = ypool.tile([P, HALF], F32, name="y%d" % g)
            elif start:
                y_bank[h, g] = zpool.tile([P, HALF], F32, name="z")
            nc.tensor.matmul_mx(
                y_bank[h, g][:, cols],
                lhsT=w4w[:, f, 2 * P * g : 2 * P * (g + 1)].bitcast(FP4X4),
                lhsT_scale=w4s[:, f, P * g : P * (g + 1)],
                rhs=h_codes[f][h][:, cols].bitcast(FP8X4),
                rhs_scale=h_scales[f][h][:, cols],
                start=start,
                stop=stop,
            )

        def copy_y(h, g):
            nc.scalar.activation(
                y_sb[g][:, HALF * h : HALF * (h + 1)], y_bank[h, g][:], ACT.Copy, scale=ga_sb[:, g : g + 1]
            )

        for a in range(2):
            round_weight(SIN, a, 0, nc.vector.tensor_copy)
            round_weight(SIN, a, 1, nc.scalar.copy)
            load_weight(*divmod(3 + a, 2))
            quantize_weight(SIN, a, 0, 2)
            quantize_weight(SIN, a, 2, 4)

        chunks = [(f, c) for f in range(3) for c in range(S // CHUNK)]
        steps = len(chunks)
        whole = slice(0, HALF)
        v2_words = keep.tile([P, PICKS], U32, name="v2_words", align_bytes=64)
        for i in range(steps + 2):
            if i < steps:
                features(*chunks[i])
            if 1 <= i <= steps:
                apply_gain(*chunks[i - 1])
            if i >= steps:
                f, c = chunks[i - 2]
                quantize_h(f, CHUNK * c, CHUNK * (c + 1))
            elif i >= 2 and i % 2 == 1:
                f, c = chunks[i - 2]
                quantize_h(f, CHUNK * (c - 1), CHUNK * (c + 1))

            if i == 0:
                for u in range(2):
                    round_weight_on_gpsimd(TANH, 0, u)
                load_weight(EXP, 1)
                quantize_weight(TANH, 0, 0, 4)
            if i == 1:
                for u in range(2):
                    round_weight(TANH, 1, u, nc.scalar.copy)
                table2 = placed([P, TB], I32, "table2", slot[0])
                nc.sync.dma_start(table2[:], tab2_words[0].rearrange("p t i -> p (t i)").bitcast(I32))
                quantize_weight(TANH, 1, 0, 4)
            if i == 2:
                for u in range(2):
                    round_weight(EXP, 0, u, nc.scalar.copy)
                w5w = placed([P, N], I32, "w5w", slot[1])
                nc.sync.dma_start(w5w[:], w5_words[0].rearrange("p t i -> p (t i)").bitcast(I32))
            if i == 4:
                for u in range(2):
                    round_weight(EXP, 1, u, nc.scalar.copy)
                w5s = placed([P, N], U8, "w5s", slot[2] + TB)
                ga_sb = placed([P, 4], F32, "ga_sb", slot[2] + TB + N)
                gb_sb = placed([P, 4], F32, "gb_sb", slot[2] + TB + N + 64)
                nc.gpsimd.memset(w5s[:].bitcast(I32), 0)
                with nc.allow_non_contiguous_dma(reason="one factor for each output row, a row to a partition"):
                    nc.sync.dma_start(ga_sb[:], ga.rearrange("(g p) -> p g", p=P))
                    nc.sync.dma_start(gb_sb[:], gb.rearrange("(g p) -> p g", p=P))
                for q in range(4):
                    nc.sync.dma_start(
                        w5s[32 * q : 32 * q + 4, :].bitcast(I32), w5_scales[0, 4 * q : 4 * q + 4, :].bitcast(I32)
                    )
            if i in (5, 6):
                quantize_weight(EXP, i - 5, 0, 4)

            if i >= 2 and chunks[i - 2][1] == 1:
                f = chunks[i - 2][0]
                for g in range(4):
                    second_pass(0, g, f, whole, f == SIN, f == EXP)
                if f == EXP:
                    copy_y(0, 0)
            if i == steps:
                for g in range(4):
                    second_pass(1, g, SIN, whole, True, False)
                    second_pass(1, g, TANH, whole, False, False)
                    second_pass(1, g, EXP, slice(0, CHUNK), False, False)
        for g in range(4):
            second_pass(1, g, EXP, slice(CHUNK, HALF), False, True)
            if g > 0:
                copy_y(0, g)
            copy_y(1, g)

        nc.vector.tensor_copy(v2_words[:], table2[:].bitcast(U32).indirect(idx2[:]))
        b_bank = []
        for g in range(4):
            b = ypool.tile([P, PICKS], F32, name="y%d" % g)
            nc.tensor.matmul_mx(
                b[:],
                lhsT=w5w[:, P * g : P * (g + 1)].bitcast(FP8X4),
                lhsT_scale=w5s[:, P * g : P * (g + 1)],
                rhs=v2_words[:].bitcast(FP8X4),
                rhs_scale=v2_scales[:],
                start=True,
                stop=True,
            )
            b_bank.append(b)

        pieces = [(g, 0, PICKS) for g in range(3)] + [(3, 0, PICKS // 2), (3, PICKS // 2, PICKS)]
        picked = []
        for i in range(len(pieces) + 1):
            if i < len(pieces):
                g, j0, j1 = pieces[i]
                y_picked = ring.tile([P, j1 - j0], F32, name="y_picked")
                nc.vector.tensor_copy(y_picked[:], y_sb[g][:].indirect(p1[:, j0 // 16 : j1 // 16]))
                picked.append(y_picked)
            if i >= 1:
                g, j0, j1 = pieces[i - 1]
                result = keep.tile([P, j1 - j0], F32, name="result%d" % (i - 1))
                nc.vector.scalar_tensor_tensor(
                    result[:], b_bank[g][:, j0:j1], gb_sb[:, g : g + 1], picked[i - 1][:], ALU.mult, ALU.max
                )
                nc.sync.dma_start(out[P * g : P * (g + 1), j0:j1], result[:])
